import numpy as np, ml_dtypes
CORES = [16,18,20,22]
N = 4
import mx_ref
BF = ml_dtypes.bfloat16
def gcols(t, e):
    v = np.concatenate([t.reshape(8, 16, -1, 4), np.zeros((8, 16, 1, 4), BF)], axis=2)
    return np.ascontiguousarray(np.stack([v[g][:, e[g]] for g in range(8)])).reshape(128, -1)
def tile(rs):
    return np.stack(rs, axis=2).reshape(128, -1).astype(BF)
def pick(q, e):
    c = np.concatenate([q[0].reshape(128, -1, 4), np.zeros((128, 1, 4), np.uint8)], axis=1); s = np.concatenate([q[1], np.ones((16, 1), np.uint8)], axis=1)
    return (np.ascontiguousarray(c[:, e].reshape(128, -1)), np.ascontiguousarray(s[:, e]))
def join(*qs):
    return (np.concatenate([q[0] for q in qs], axis=1), np.concatenate([q[1] for q in qs], axis=1))
def put(q, e, v):
    c, s = q[0].reshape(128, -1, 4).copy(), q[1].copy(); c[:, e] = v[0].reshape(128, -1, 4); s[:, e] = v[1]
    return (c.reshape(128, -1), s)
def pk(c, s):
    return (np.ascontiguousarray(c), mx_ref.live(s))
def emit(q):
    return q[0], q[1]
def packed(v, rng):
    q = [mx_ref.quantize(np.ascontiguousarray(v[r])) for r in range(N)]
    return np.stack([a for a, b in q]), np.stack([mx_ref.plane(b, rng) for a, b in q])
def values_of_codes():
    e, c = np.zeros((128, 128, 4), np.float32), np.zeros((128, 2, 4), np.uint8)
    e[np.arange(128), np.arange(128), 0] = 1
    c[:127, :, 0] = np.arange(256).reshape(2, 128).T[:127]
    return mx_ref.matmul(mx_ref.quantize(e.reshape(128, 512).astype(BF)), (c.reshape(128, 8), np.full((16, 2), 127, np.uint8))).T.reshape(-1).astype(np.float64)
CODE_VALUE, SCALE_VALUE = values_of_codes(), 2.0 ** (np.arange(256) - 127.0)
def decode(q):
    return (CODE_VALUE[q[0]].reshape(16, 8, -1, 4) * SCALE_VALUE[q[1]][:, None, :, None] + 0.0).reshape(128, -1).astype(np.float32)
def f(rng, *shape):
    return mx_ref.flush((rng.standard_normal(shape, dtype=np.float32) * np.exp2(rng.integers(-2, 3, shape[:-1] + (1,)))).astype(BF))
def wide(rng, *shape, cols=0):
    v = rng.standard_normal(shape, dtype=np.float32) * np.exp2(rng.integers(-12, 13, shape)).astype(np.float32)
    if cols: v *= np.repeat(np.exp2(rng.integers(-cols, cols + 1, shape[:-2] + (1, shape[-1] // 4))) * (rng.random(shape[:-2] + (1, shape[-1] // 4)) > 0.0625), 4, axis=-1).astype(np.float32)
    return mx_ref.flush(v.astype(BF))
C, S = 448, 112
def order(p):
    return np.argsort(-(p[::16] + np.float32(0.0)), axis=1, kind="stable")
def places(o):
    return np.argsort(o, axis=1)
def numbers_of(rng):
    return {"x": np.array(f(rng, N, 128, 4 * C)), "u": np.array(f(rng, N, 128, 512)), "v": np.array(f(rng, N, 128, 512)), "m": np.array(f(rng, N, 128, 512))}
def weights(rng, w):
    c, p = packed(w, rng)
    return {"wc": c, "ws": p}
def unit(rng, a, b, low=False):
    w = np.zeros((N, 128, 4, 128, 4), np.float32)
    i = np.arange(128)
    j = i[i % 16 // 4 == 2]
    for k in range(4):
        w[:, i, k, i, k] = np.where(i % 16 < 8, a, b)
        if low: w[:, j + 4, k, j, k] = b
    return weights(rng, w.reshape(N, 128, 2048).astype(BF))
def signs(rng):
    return np.stack([rng.permutation(8) % 2 * 2.0 - 1.0 for r in range(N)])
def digits(s):
    return np.stack([s // 64 * 64, s // 8 % 8 * 8, s % 8, 0 * s], axis=-1)
def setup_inputs(rng):
    return {**numbers_of(rng), **weights(rng, f(rng, N, 128, 2048))}
def setup_inputs_ties(rng):
    d = numbers_of(rng)
    e = rng.permutation(N)
    x = d["x"].reshape(N, 8, 16, C, 4)
    for r in range(N):
        k = np.zeros(C, int) if r == e[0] else rng.permutation(C) % 3
        a = np.abs(x[r][:, :8, :3].astype(np.float32))
        a[:, :, 2] = 0
        x[r][:, :8] = a[:, :, k].astype(BF)
        if r == e[2]:
            z = np.flatnonzero(k == 2)
            n = int(rng.integers(0, len(z) - 15))
            x[r][:, :, z[n:n + 16]] = 0
    x[e[1]][:, :8] = x[e[0]][:, :8]
    u, v = d["u"].reshape(N, 8, 16, 128, 4), d["v"].reshape(N, 8, 16, 128, 4)
    u[:, :, 8:, ::16] = 0
    v[:, :, 8:, ::16] = 0
    w = np.array(f(rng, N, 128, 2048)).astype(np.float32).reshape(N, 8, 16, 4, 8, 16, 4)
    w[:, :, 8:, :, :, :8] = 0
    w[:, :, :8, :, :, 8:] = 0
    w[:, :, :8, :, :, :8] = 0.0 - np.abs(w[:, :, :8, :, :, :8])
    return {"x": x.reshape(N, 128, 4 * C), "u": u.reshape(N, 128, 512), "v": v.reshape(N, 128, 512), "m": d["m"], **weights(rng, w.reshape(N, 128, 2048).astype(BF))}
def setup_inputs_near(rng):
    d = numbers_of(rng)
    x = d["x"].astype(np.float32).reshape(N, 8, 16, C, 4)
    s = (np.arange(C) // 2 + rng.integers(0, C // 2, (N, 8, 1))) % (C // 2)
    g = ((s[..., None] >> np.arange(8)) & 1) * np.exp2(np.arange(8) - 23.0)
    x[:, :, 0] = 0
    x[:, :, 0, :, 0] = -1
    x[:, :, 8] = 0.0 - g[..., :4]
    x[:, :, 9] = 0.0 - g[..., 4:]
    x[:, :, 10:] = rng.integers(4, 8, (N, 8, 6, C, 4)) * rng.choice([-1.0, 1.0], (N, 8, 6, C, 4)) * 2.0 ** -20
    x = x * np.float32(2.0 ** 16)
    u, v = d["u"].reshape(N, 128, 128, 4), d["v"].reshape(N, 128, 128, 4)
    u[:, :, ::16] = 0
    v[:, :, ::16] = 0
    a, b = (signs(rng) * -2.0 ** -30).astype(np.float32).astype(BF), (signs(rng) * -2.0 ** -30).astype(np.float32).astype(BF)
    for h in range(0, 128, 16):
        u[:, h, h, 0] = a[:, h // 16]
        v[:, h, h, 0] = b[:, h // 16]
        u[:, h + 8:h + 10, h] = -2.0 ** -30
        v[:, h + 8:h + 10, h] = 2.0 ** -30
    return {"x": x.reshape(N, 128, 4 * C).astype(BF), "u": u.reshape(N, 128, 512), "v": v.reshape(N, 128, 512), "m": d["m"], **unit(rng, 256, 256)}
def setup_inputs_huge(rng):
    d = numbers_of(rng)
    x = np.zeros((N, 8, 16, C, 4))
    e = rng.permutation(N)
    one = rng.permutation(N) < N // 2
    both = rng.permutation(N // 2) % 2
    for r in range(N):
        s = np.ones(N) if one[r] else rng.permutation(N) % 2 * 2.0 - 1.0
        val = np.sort(np.r_[0.875, 1 + 0.125 * np.arange(N - 1)] * 2.0 ** 29 * s)[::-1]
        lev = rng.permutation(C) % N
        x[r][:, :8] = val[lev][:, None]
        x[r][:, 8:] = 2.0 ** 13 * (0.5 + 0.5 * rng.random((8, 8, C, 4)))
        h = np.sort(rng.permutation(S)[:2])
        for l in range(N):
            j = np.flatnonzero(lev == l)[h]
            k = both[min(l, N - 1 - l)]
            if r == e[0]: x[r][:, 8:, j] = np.array([1.75, 1.625] if k else [1.625, 1.75])[:, None] * 2.0 ** 24
            if r == e[1] and k: x[r][:, 8:, j[0]] = -1.625 * 2.0 ** 24
    u, v = d["u"].reshape(N, 8, 16, 128, 4), d["v"].reshape(N, 8, 16, 128, 4)
    for t, p in ((u, slice(0, 8)), (v, slice(8, 16))):
        a = 2.0 ** 30 * (1 - 0.125 * rng.random((N, 8, 8, 8, 4))) * signs(rng)[:, None, None, :, None]
        t[:, :, :, ::16] = 0
        t[:, :, p, ::16] = a.astype(np.float32).astype(BF)
    return {"x": x.astype(np.float32).reshape(N, 128, 4 * C).astype(BF), "u": u.reshape(N, 128, 512), "v": v.reshape(N, 128, 512), "m": d["m"], **unit(rng, 0.015625, 4096)}
def setup_inputs_scan(rng):
    d = numbers_of(rng)
    i = np.arange(C)
    a = rng.integers(1, 26, (N, 8, 1))
    at = a + 26 * rng.integers(0, (C - 93) // 26 + 1, (N, 8, 1))
    two = np.stack([rng.permutation(8) < 2 for r in range(N)])[..., None]
    far = two & (i >= at) & (i < at + 68)
    n = np.where(two & (i >= at + 68), i - at - 68, i - a)
    since = np.where(far, i - at, np.where(i < a, i, n % 26))
    anew = far & (since == 40)
    quiet = (i >= a) & (n // 26 % 2 == 1)
    shape = (N, 8, C, 4, 4)
    kind = rng.choice(5, shape, p=[0.2, 0.1, 0.2, 0.35, 0.15])
    kind = np.where(quiet[..., None, None] & (kind < 3), 3, kind)
    kind = np.where(far[..., None, None], 4, kind)
    kind = np.where((since == 0)[..., None, None], 5, kind)
    kind[..., 3] = np.where(anew[..., None], 5, kind[..., 3])
    top = 16 * rng.integers(8, 13, shape) + rng.integers(7, 10, shape)
    rest = rng.integers(128, 240, shape)
    h, now = np.zeros(shape, int), np.zeros((N, 8, 4, 4), int)
    for k in range(C):
        t = kind[:, :, k]
        now = np.where(t == 5, top[:, :, k], now)
        h[:, :, k] = np.select([t == 0, t == 1, t == 2, t == 3, t == 5], [now - 1, now + 1, rest[:, :, k], -rest[:, :, k], now], 0)
        now = now + (t == 1)
    head = far & (since == 0) | anew
    size = np.where(head, np.where(anew, 2.0 ** -7, 2.0 ** 21), np.exp2(5.0 - since))[..., None, None] * np.where(kind == 2, 0.0625, 1.0)
    high = np.sign(h) * (np.abs(h) // 16 * 16)
    upper = np.where(head[..., None, None], h - high, high)
    w = np.argsort(rng.random((N, 8, C)), axis=2)
    g = np.arange(8)[:, None]
    c = S * np.arange(N)[:, None, None] + w % S
    p = np.concatenate([0.0 - digits(C - 1 - c)[..., None, :], 0.0 - digits(C - 1 - i + 0 * c)[..., None, :], upper * size, (h - upper) * size], axis=3)
    q, z = np.zeros(p.shape), np.zeros(p.shape)
    q[w // S, g, c] = p
    z[np.arange(N)[:, None, None], g, np.argsort(rng.random((N, 8, C)), axis=2)] = q
    x = d["x"].astype(np.float32).reshape(N, 8, 16, C, 4)
    x[:, :, np.r_[0:2, 8:16]] = z.transpose(0, 1, 3, 2, 4)
    u, v = d["u"].reshape(N, 128, 128, 4), d["v"].reshape(N, 128, 128, 4)
    u[:, :, ::16] = 0
    v[:, :, ::16] = 0
    for b in range(0, 128, 16):
        u[:, b, b, :3] = -1
        v[:, b + 1, b, :3] = -1
    return {"x": x.reshape(N, 128, 4 * C).astype(BF), "u": u.reshape(N, 128, 512), "v": v.reshape(N, 128, 512), "m": d["m"], **unit(rng, 256, 256, True)}
def setup_inputs_spread(rng):
    d = setup_inputs(rng)
    x = wide(rng, N, 128, 4 * C).astype(np.float32).reshape(N, 128, C, 4)
    x = x * np.exp2(rng.integers(-6, 7, (N, 1, C, 1))).astype(np.float32)
    for r in range(N): x[r][:, rng.permutation(C)[:24 // N]] = 0
    d["x"] = mx_ref.flush(x.reshape(N, 128, 4 * C).astype(BF))
    return d
def scanned(x, u, v, wc, ws):
    first, second, out, value = [], [], [], []
    run = np.arange(S)
    for r in range(N):
        o = order(mx_ref.matmul(mx_ref.quantize(u[r]), mx_ref.quantize(x[r])))
        first.append(o)
        out.append(mx_ref.quantize(gcols(x[r], o)))
    for d in range(N):
        w = pk(wc[d], ws[d])
        a = join(*[pick(out[r], S * d + run) for r in range(N)])
        h = tile([mx_ref.matmul(pick(w, np.arange(128 * b, 128 * b + 128)), a) * np.float32(0.00390625) for b in range(4)])
        o = order(mx_ref.matmul(mx_ref.quantize(v[d]), mx_ref.quantize(h)))
        second.append(o)
        s = gcols(h, o).astype(np.float32).reshape(128, C, 4)
        s[:, 0] = np.maximum(s[:, 0], np.float32(0.0))
        for i in range(1, C): s[:, i] = np.maximum(s[:, i - 1] * np.float32(0.5), s[:, i])
        value.append(s + np.float32(0.0))
    return first, second, value
def check_inputs(d):
    b = []
    for k in ("x", "u", "v", "m"):
        a = np.abs(d[k].astype(np.float32))
        if not (np.isfinite(a).all() and ((a == 0) | (a >= 2.0 ** -30) & (a <= 2.0 ** 30)).all()): b.append("a value of " + k)
    return b
def reference(x, u, v, m, wc, ws):
    first, second, value = scanned(x, u, v, wc, ws)
    back = [mx_ref.quantize(gcols(value[d].reshape(128, 4 * C).astype(BF), places(second[d]))) for d in range(N)]
    run = np.arange(S)
    y, oa, ob = np.zeros((N, 128, C), np.float32), np.zeros((N, 8, C), np.float32), np.zeros((N, 8, C), np.float32)
    oc, osc = np.zeros((N, 128, 4 * C), np.uint8), np.zeros((N, 16, C), np.uint8)
    for r in range(N):
        b = decode(join(*[pick(back[d], S * r + run) for d in range(N)])).astype(BF)
        z = gcols(b, places(first[r])).astype(np.float32) + x[r].astype(np.float32)
        q = mx_ref.quantize(z.astype(BF))
        y[r] = mx_ref.matmul(mx_ref.quantize(m[r]), q)
        oa[r], ob[r] = first[r], second[r]
        oc[r], osc[r] = emit(q)
    return {"y": y, "oa": oa, "ob": ob, "oc": oc, "osc": osc}

@@ -1,0 +1,433 @@
+from concourse.bass import DstId, RemoteDMATransfer
+from concourse.mybir import dt, AluOpType as A, ActivationFunctionType as F
+
+C, S, N = 448, 112, 4
+KB = C // 16
+KV = 12
+KS = KB - KV
+CV, CS = 16 * KV, 16 * KS
+HC, HB = C // 2, KB // 2
+ZP = [0, 14, 28]
+GS, GV = 4, 4
+X4, U8, BF, F32 = "float8_e4m3fn_x4", "uint8", "bfloat16", "float32"
+
+SCRATCH = {
+    "xt": ("sbuf", [128, 4 * C], BF), "ut": ("sbuf", [128, 512], BF), "vt": ("sbuf", [128, 512], BF), "mt": ("sbuf", [128, 512], BF),
+    "xp": ("sbuf", [128, 4 * C], BF), "ft": ("sbuf", [128, 4 * C], BF), "ht": ("sbuf", [128, 4 * C], BF), "hp": ("sbuf", [128, 4 * C], BF),
+    "hs": ("sbuf", [128, 4 * C], BF), "rs": ("sbuf", [128, 4 * C], BF), "tt": ("sbuf", [128, 4 * C], BF),
+    "zs": ("sbuf", [128, 4 * C], BF), "zt": ("sbuf", [128, 4 * C], BF),
+    "ones": ("sbuf", [128, 512], BF), "et": ("sbuf", [128, 2048], BF),
+    "sp": ("sbuf", [128, C + 16], F32), "turn": ("sbuf", [128, 928], F32), "dpos": ("sbuf", [128, 32], F32), "dneg": ("sbuf", [128, 32], F32),
+    "eq": ("sbuf", [128, C], BF), "eqs": ("sbuf", [128, C], BF), "after": ("sbuf", [128, C], BF), "cidx": ("sbuf", [128, C], BF),
+    "vals": ("sbuf", [128, C], BF), "half": ("sbuf", [128, C], BF),
+    "cst": ("sbuf", [128, KB], F32), "cc": ("sbuf", [128, KB], BF),
+    "mask": ("sbuf", [128, KV * C], BF), "sgn": ("sbuf", [128, KS * CS], BF), "sums": ("sbuf", [128, KV * HC], BF),
+    "cols": ("sbuf", [128, KV * (CS + 32)], BF), "colt": ("sbuf", [128, 2 * CS + 32], BF), "colu": ("sbuf", [128, 2 * CS + 32], BF),
+    "cap1": ("sbuf", [128, KV * CS], BF), "cap2": ("sbuf", [128, 2 * CS + 32], BF),
+    "acc": ("sbuf", [128, 3 * KS], F32), "acce": ("sbuf", [128, 3 * KS], F32), "turns": ("sbuf", [128, 3 * KS + 3], F32),
+    "inv": ("sbuf", [128, 960], BF), "invt": ("sbuf", [128, 928], BF),
+    "oaf": ("sbuf", [128, C], F32), "obf": ("sbuf", [128, C], F32), "yf": ("sbuf", [128, C], F32),
+    "i16": ("sbuf", [128, KB], "int32"), "cx": ("sbuf", [128, 128], F32), "cxt": ("sbuf", [128, 128], F32),
+    "l_u": ("sbuf", [128, 8], "uint16"), "l_d": ("sbuf", [128, 4], "uint16"), "l_rep": ("sbuf", [128, KB], "uint16"),
+    "l_own": ("sbuf", [128, 8], "uint16"), "l_col": ("sbuf", [128, 2], "uint16"),
+    "place1": ("sbuf", [128, KB], "uint16"), "place2": ("sbuf", [128, KB], "uint16"),
+    "order1": ("sbuf", [128, 32], "uint16"), "order2": ("sbuf", [128, 32], "uint16"),
+    "ps": ("psum", [128, 4096], F32),
+}
+for _n, _w in (("x", C), ("u", 128), ("ur", 128), ("v", 128), ("vr", 128), ("m", 128), ("w", 512), ("e", 512),
+               ("f", C), ("a", C), ("h", C), ("t", C), ("b", C), ("z", C)):
+    SCRATCH[_n + "_q"] = ("sbuf", [128, _w], X4)
+    SCRATCH[_n + "_s"] = ("sbuf", [128, _w], U8)
+
+POOL = ["e%d" % i for i in range(110)]
+LOADS = ["ld%d" % i for i in range(8)]
+SEMAPHORES = POOL + LOADS + ["far_a", "near_a", "far_b", "near_b", "sent", "outs"]
+
+
+def engine_plan(T, topo, r):
+    src = T.cores[r]
+    far = [d for d in range(N) if d // 2 != r // 2]
+    near = [d for d in range(N) if d // 2 == r // 2 and d != r][0]
+    eng = [e for e in topo.engines(src, T.cores[near]) if all(e in topo.engines(src, T.cores[d]) for d in far)]
+    q = len(eng) // 2
+    return [{far[0]: eng[:q], far[1]: eng[q:]}, {near: eng}]
+
+
+def rank_program(g, core, T, topo):
+    rank = T.rank_of(core)
+    if rank is None:
+        return
+    Q = {"g": g, "v": g.vector, "s": g.scalar, "t": g.tensor, "y": g.sync}
+    V, SC, PE = g.vector, g.scalar, g.tensor
+    late = rank // 2
+    early = 1 - late
+
+    known = {q: set() for q in Q}
+    events = []
+    total, last_on, waited = {}, {}, {}
+    writer, readers = {}, {}
+    loads = list(LOADS)
+
+    def wait(q, e):
+        if e in known[q]:
+            return
+        s, n, k = events[e]
+        Q[q].wait_ge(T.sem[s], n)
+        waited[s] = max(waited.get(s, 0), n)
+        known[q].add(e)
+        known[q].update(k)
+
+    def op(q, make, reads=(), writes=(), join=None, load=False, out=False):
+        need = set()
+        for k in reads:
+            if k in writer:
+                need.add(writer[k])
+            if k.startswith("ps"):
+                need.update(e for e, qq in readers.get(k, []) if qq != q)
+        for k in writes:
+            if k in writer:
+                need.add(writer[k])
+            need.update(e for e, qq in readers.get(k, []))
+        need.discard(join)
+        for e in sorted(need, reverse=True):
+            wait(q, e)
+        if out:
+            make().then_inc(T.sem.outs, 16)
+            total["outs"] = total.get("outs", 0) + 16
+            return None
+        step = 16 if load else 1
+        if join is None:
+            if load:
+                s = loads.pop(0)
+            else:
+                free = [x for x in POOL if x in last_on and last_on[x] in known[q]]
+                s = min(free, key=lambda x: last_on[x]) if free else [x for x in POOL if x not in last_on][0]
+            e = len(events)
+            events.append([s, 0, set()])
+            last_on[s] = e
+        else:
+            e = join
+            s = events[e][0]
+        make().then_inc(T.sem[s], step)
+        total[s] = total.get(s, 0) + step
+        events[e][1] = total[s]
+        events[e][2].update(known[q])
+        for k in reads:
+            readers.setdefault(k, []).append((e, q))
+        for k in writes:
+            writer[k] = e
+            readers[k] = []
+        return e
+
+    def bank(i, a=0, b=HC):
+        return T.ps[:, 512 * i + a:512 * i + b]
+
+    def u8(ap):
+        return ap.bitcast(dt.uint8)
+
+    def u32(ap):
+        return ap.bitcast(dt.uint32)
+
+    def quant(name, src, a, b, reads, writes):
+        return op("v", lambda: V.quantize_mx(T[name + "_q"][:, a:b], T[name + "_s"][:, a:b], src[:, 4 * a:4 * b]), reads, writes)
+
+    def mm(i, w, wa, x, a, b, reads):
+        return op("t", lambda: PE.matmul_mx(bank(i, 0, b - a), T[w + "_q"][:, wa:wa + 128], T[w + "_s"][:, wa:wa + 128],
+                                            T[x + "_q"][:, a:b], T[x + "_s"][:, a:b], True, True), reads, ["ps%d" % i])
+
+    def pick(dst, a, b, src, width, lst, reads, key):
+        op("v", lambda: V.tensor_copy(u32(T[dst + "_q"][:, a:b]), u32(T[src + "_q"][:, 0:width]).indirect(lst)), reads, [key + "q"])
+        op("s", lambda: SC.activation(T[dst + "_s"][:, a:b], T[src + "_s"][:, 0:width].indirect(lst), F.Copy), reads, [key + "s"])
+
+    def move(q, out, in_, reads, writes):
+        if q == "v":
+            return op("v", lambda: V.tensor_copy(out, in_), reads, writes)
+        return op("s", lambda: SC.activation(out, in_, F.Copy), reads, writes)
+
+    def turn(out, in_, reads, writes, join=None):
+        return op("v", lambda: V.transpose(out, in_), reads, writes, join=join)
+
+    def elem(t, b, a=0, z=C):
+        return t[:, 4 * a + b:4 * z:4]
+
+    def plane(t, b, a=0, z=C):
+        return t[:, C * b + a:C * b + z]
+
+    def gather(q, dst, src, b, lst, a, z, reads, key):
+        move(q, elem(dst, b, 16 * a, 16 * z), plane(src, b).indirect(T[lst][:, a:z]), reads, [key])
+
+    op("s", lambda: SC.dma_start(T.ut[:], T.u[:]), [], ["ut"], load=True)
+    op("y", lambda: g.sync.dma_start(T.xt[:, 0:2 * C], T.x[:, 0:2 * C]), [], ["xt0"], load=True)
+    op("y", lambda: g.sync.dma_start(T.xt[:, 2 * C:4 * C], T.x[:, 2 * C:4 * C]), [], ["xt1"], load=True)
+    XT = ["xt0", "xt1"]
+    op("y", lambda: g.sync.dma_start(T.vt[:], T.v[:]), XT, ["vt"], load=True)
+    op("y", lambda: g.sync.dma_start(u8(T.w_q[:]), T.wc[:]), [], ["wq"], load=True)
+    op("y", lambda: g.sync.dma_start(T.w_s[:], T.ws[:]), [], ["ws"], load=True)
+    op("y", lambda: g.sync.dma_start(T.mt[:], T.m[:]), [], ["mt"], load=True)
+
+    def iota(out, pattern, base, key):
+        op("g", lambda: g.iota(out, pattern, base, 0, allow_small_or_imprecise_dtypes=True), [], [key])
+
+    op("g", lambda: g.iota(T.i16[:], [[16, KB]], 0, 0), [], ["i16"])
+    for a, far, base in ((0, C + 16, 0), (32, C + 16, 0), (96, CS + 16, 15)):
+        iota(T.cx[:, a:a + 16], [[32, 8], [16 + far, 2]], base, "cx%da" % a)
+        iota(T.cx[:, a + 16:a + 32], [[32, 8], [16 - far, 2]], base + far, "cx%db" % a)
+    iota(T.cx[:, 64:96], [[0, 2], [1, 16]], 0, "cx64")
+    iota(T.cidx[:], [[0, KB], [1, 16]], 0, "cidx")
+    iota(T.vals[:], [[1, C]], -HC, "vals")
+    iota(T.turns[:], [[0, KS + 1], [1, 3]], -1, "turns")
+    iota(T.cap1[:], [[0, CS], [1, KV]], 0, "cap1")
+    iota(T.cap2[:], [[0, 2 * KS + 2], [KV, 16]], 0, "cap2")
+
+    op("v", lambda: V.memset(T.turn[:, 448:480], 0.0), [], ["turnpad"])
+    op("v", lambda: V.memset(T.acc[:], 0.0), [], ["accu%d" % k for k in range(KS)] + ["accl%d" % k for k in range(KS)] + ["accc"])
+    op("v", lambda: V.memset(T.cst[:, 0:KV], -HC - 1.0), [], ["cstv"])
+    op("v", lambda: V.memset(T.inv[:], 0.0), [], ["inv0", "inv1"])
+    op("v", lambda: V.memset(T.cols[:, 0:CV], 0.0), [], ["colpad0"])
+    op("v", lambda: V.memset(T.cols[:, CV + KV * CS:2 * CV + KV * CS], 0.0), [], ["colpad1"])
+    op("v", lambda: V.memset(T.ones[:], 1.0), [], ["ones"])
+    op("v", lambda: V.tensor_copy(T.l_u[:], T.i16[:, 0:8]), ["i16"], ["l_u"])
+    op("v", lambda: V.tensor_scalar(T.l_rep[:], T.i16[:], 0.0625, None, A.mult), ["i16"], ["l_rep"])
+    op("v", lambda: V.tensor_scalar(T.cst[:, KV:KB], T.i16[:, KV:KB], 15.0 - HC, None, A.add), ["i16"], ["csts"])
+    op("v", lambda: V.memset(T.cx[:, 16:17], 912.0), [], ["cx0b"])
+    turn(T.cxt[:], T.cx[:], ["cx0a", "cx0b", "cx32a", "cx32b", "cx96a", "cx96b", "cx64"], ["cxt"])
+    op("v", lambda: V.tensor_copy(T.l_d[:, 0:3:2], T.cxt[:, 0:33:32]), ["cxt"], ["l_d0"])
+    op("v", lambda: V.tensor_scalar(T.l_d[:, 1:4:2], T.cxt[:, 32:34], 256.0, 927.0, A.add, A.min), ["cxt"], ["l_d1"])
+    op("v", lambda: V.tensor_copy(T.l_col[:], T.cxt[:, 96:98]), ["cxt"], ["l_col"])
+    op("v", lambda: V.tensor_scalar(T.l_own[:, 0:7], T.i16[:, 0:7], T.cxt[:, 64:65], float(S * rank), A.add, A.add), ["i16", "cxt"], ["l_own"])
+    for b in range(4):
+        op("g", lambda b=b: g.affine_select(T.et[:, 512 * b:512 * b + 512], T.ones[:], [[1, 512]], A.is_equal, 0.0, -b, -4),
+           ["ones"], ["et%d" % b])
+
+    def scores(w, x, h, last, reads):
+        a, i = HC * h, 6 if last else 4
+        mm(i, w, 0, x, a, a + HC, reads)
+        mm(i + 1, w, 0, x, a, a + HC, reads)
+        if h == 0:
+            move("s", T.sp[:, C:C + 16], bank(i + 1, 0, 16), ["ps%d" % (i + 1)], ["spx"])
+        move("s", T.sp[:, a:a + HC], bank(i + 1), ["ps%d" % (i + 1)], ["sp%d" % h])
+        e = turn(T.turn[:, a:a + HC], bank(i), ["ps%d" % i], ["turna%d" % h])
+        turn(T.turn[:, 480 + a:672 + a], bank(i, 16, 208), ["ps%d" % i], ["turnb%d" % h], join=e)
+        if last:
+            turn(T.turn[:, 896:928], T.sp[:, 432:464], ["sp1", "spx"], ["turnd"], join=e)
+            turn(T.turn[:, 672:704], T.sp[:, 208:240], ["sp0", "sp1"], ["turnc"], join=e)
+
+    def rank_columns(place, order, slot):
+        turned = ["turna0", "turna1", "turnb0", "turnb1", "turnc", "turnd", "turnpad", "l_d0", "l_d1"]
+        SP = ["sp0", "sp1"]
+        one = {}
+
+        def joined(name, q, make, reads, writes):
+            one[name] = op(q, make, reads, writes, join=one.get(name))
+
+        op("s", lambda: SC.activation(T.dneg[:], T.turn[:, 0:928].indirect(T.l_d[:, 0:2]), F.Identity, scale=-1.0), turned, ["dneg"])
+        move("v", T.dpos[:], T.turn[:, 0:928].indirect(T.l_d[:, 0:2]), turned, ["dpos"])
+
+        def sign(k):
+            joined(("sign", k // GS), "s",
+                   lambda: SC.activation(T.sgn[:, CS * k:CS * k + CS], T.sp[:, CV:C], F.Sign, bias=T.dneg[:, KV + k:KV + k + 1]),
+                   SP + ["dneg"], ["sgl%d" % k, "sgu%d" % k])
+
+        def count(k):
+            a, n = CS * k, 16 * k + 16
+            lo, up = T.sgn[:, a:a + n], T.sgn[:, a + n:a + CS]
+            joined("count", "s", lambda: SC.activation(lo, lo, F.Relu, scale=-1.0, accum_out=T.acc[:, 3 * k + 1:3 * k + 2]),
+                   [], ["sgl%d" % k, "accl%d" % k])
+            if n < CS:
+                joined("count", "s", lambda: SC.activation(up, up, F.Relu, accum_out=T.acc[:, 3 * k + 2:3 * k + 3]),
+                       [], ["sgu%d" % k, "accu%d" % k])
+
+        for k in range(KS + GS + 1):
+            if k < KS:
+                sign(k)
+            if k > GS:
+                count(k - GS - 1)
+
+        def row(k, a, z):
+            return T.mask[:, KV * a + k:KV * z:KV]
+
+        def compare(k):
+            n = 16 * k + 16
+            for a, z, how, name in ((0, n, A.is_ge, "ml%d"), (n, C, A.is_gt, "mu%d")):
+                joined(("mask", k // GV), "v", lambda: V.tensor_scalar(row(k, a, z), T.sp[:, a:z], T.dpos[:, k:k + 1], None, how),
+                       SP + ["dpos"], [name % k])
+
+        def add_up(k):
+            joined("sum", "v", lambda: V.tensor_tensor_scan(T.sums[:, HC * k:HC * k + HC], row(k, 0, HC), row(k, HC, C), T.cc[:, k:k + 1],
+                                                            A.add, A.add), ["ml%d" % k, "mu%d" % k, "cc"], ["sum%d" % k])
+
+        o = 480 * slot
+        key = "inv%d" % slot
+
+        def scatter(a, z, part):
+            op("v", lambda: V.tensor_copy(T.inv[:, o + 16:o + 16 + C].indirect(T[place][:, a:z]), T.vals[:, 16 * a:16 * z]), [part, "vals"], [key])
+
+        op("v", lambda: V.tensor_tensor(T.eq[:], T.dpos[:, 0:32].indirect(T.l_rep[:, 0:KB]), T.sp[:, 0:C], A.is_equal),
+           SP + ["dpos", "l_rep"], ["eq"])
+        compare(0)
+        op("v", lambda: V.tensor_tensor_scan(T.eqs[:], T.eq[:], T.after[:], 0.0, A.add, A.mult), ["eq", "after"], ["eqs"])
+        compare(1)
+        op("v", lambda: V.tensor_tensor(T.cc[:], T.cst[:], T.eqs[:, 15:C:16], A.subtract), ["cstv", "csts", "eqs"], ["cc"])
+        for k in range(2, KV):
+            compare(k)
+            if k > GV:
+                add_up(k - GV - 1)
+        for k in range(KV - GV - 1, KV - 1):
+            add_up(k)
+        op("v", lambda: V.tensor_tensor_scan(T.cols[:, CV:CV + KV * CS], T.cap1[:], T.mask[:, KV * CV:KV * C], 0.0, A.min, A.add),
+           ["cap1"] + ["mu%d" % k for k in range(KV)], ["cols"])
+        add_up(KV - 1)
+        e = turn(T.colt[:, 0:CS], T.cols[:, CV + KV - 1:CV + KV * CS:KV], ["cols"], ["colt1"])
+        turn(T.colt[:, CS:2 * CS + 32], T.cols[:, KV - 1:KV * (CS + 32):KV], ["cols", "colpad0", "colpad1"], ["colt2"], join=e)
+        op("v", lambda: V.tensor_scalar(T[place][:, 0:KV], T.sums[:, HC - 1:HC * KV:HC], float(HC), None, A.add),
+           ["sum%d" % k for k in range(KV)], [place + "v"])
+        op("v", lambda: V.tensor_tensor_scan(T.colu[:], T.cap2[:], T.colt[:], 0.0, A.min, A.add), ["cap2", "colt1", "colt2"], ["colu"])
+        scatter(0, KV - 2, place + "v")
+        op("v", lambda: V.tensor_tensor(T.acc[:, 0:3 * KS:3], T.colu[:, 0:2 * CS + 32].indirect(T.l_col[:, 0:1]), T.cc[:, KV:KB], A.subtract),
+           ["colu", "l_col", "cc"], ["accc"])
+        scatter(KV - 2, KV, place + "v")
+        op("v", lambda: V.tensor_tensor_scan(T.acce[:], T.turns[:, 1:3 * KS + 1], T.acc[:], 0.0, A.mult, A.add),
+           ["accu%d" % j for j in range(KS)] + ["accl%d" % j for j in range(KS)] + ["accc", "turns"], ["acce"])
+        op("v", lambda: V.tensor_scalar(T[place][:, KV:KB], T.acce[:, 2:3 * KS:3], float(HC), None, A.add), ["acce"], [place + "s"])
+        scatter(KV, KB, place + "s")
+        e = turn(T.invt[:, 0:448], T.inv[:, o + 16:o + 464], [key], ["invt1"])
+        turn(T.invt[:, 448:928], T.inv[:, o:o + 480], [key], ["invt2"], join=e)
+        op("v", lambda: V.tensor_scalar(T[order][:], T.invt[:, 0:928].indirect(T.l_d[:, 2:4]), float(HC), None, A.add),
+           ["invt1", "invt2", "l_d0", "l_d1"], [order])
+
+    def store_order(slot, buf, out):
+        o = 480 * slot
+        op("s", lambda: SC.activation(T[buf][:], T.inv[:, o + 16:o + 16 + C], F.Identity, bias=float(HC)), ["inv%d" % slot], [buf])
+        for k in range(8):
+            op("y", lambda k=k: g.sync.dma_start(out[k:k + 1, :], T[buf][16 * k:16 * k + 1, :]), [buf], out=True)
+
+    plan = engine_plan(T, topo, rank)
+    arrive = [sum(2 * len(engine_plan(T, topo, r)[i].get(rank, ())) for r in range(N) if r != rank) for i in range(2)]
+
+    def send(src, dst, i, key):
+        wait("g", writer[key])
+        for suffix, view in (("_q", u8), ("_s", lambda ap: ap)):
+            ts = []
+            for d, engines in plan[i].items():
+                rid, pid, _ = topo.addr(T.cores[d])
+                ts.append(RemoteDMATransfer(dst_ids=[DstId(rid=rid, pnc=pid)], dma_engine_mask=sum(1 << x for x in engines),
+                                            remote_sem=T.sem[("far_", "near_")[i] + dst], src=view(T[src + suffix][:, S * d:S * d + S]),
+                                            dst=view(T[dst + suffix][:, S * rank:S * rank + S])))
+                total["sent"] = total.get("sent", 0) + len(engines)
+            g.remote_dma_fused(ts, local_sem=T.sem.sent)
+
+    def keep(src, dst):
+        pick(dst, S * rank, S * rank + S, src, C, T.l_own[:, 0:7], [src + "q0", src + "q1", "l_own"], dst)
+
+    def products(w, x, h, blocks, reads):
+        a = HC * h
+        PE.wait_ge(T.sem[("far_" if h == early else "near_") + x], arrive[0 if h == early else 1])
+        first = 4 if h == early else 0
+        for b in blocks:
+            mm(first + b, w, 128 * b, x, a, a + HC, reads + ([x + "q", x + "s"] if h == late else []))
+        return a, first
+
+    quant("u", T.ut, 0, 128, ["ut"], ["uq"])
+    pick("ur", 0, 128, "u", 128, T.l_u[:, 0:8], ["uq", "l_u"], "ur")
+    op("v", lambda: V.tensor_scalar(T.after[:], T.cidx[:], T.cxt[:, 64:65], None, A.is_gt), ["cidx", "cxt"], ["after"])
+    for h in range(2):
+        quant("x", T.xt, HC * h, HC * h + HC, ["xt%d" % h], ["xq%d" % h])
+        scores("ur", "x", h, h == 1, ["urq", "urs", "xq%d" % h])
+    rank_columns("place1", "order1", 0)
+    for b in (0, 1, 2, 3):
+        move("s", plane(T.xp, b), elem(T.xt, b), XT, ["xp%d" % b])
+
+    for i, h in enumerate((early, late)):
+        for q, b in (("v", 0), ("s", 1), ("v", 2), ("s", 3)):
+            gather(q, T.ft, T.xp, b, "order1", HB * h, HB * h + HB, ["xp%d" % b, "order1"], "ft%d%d" % (h, b))
+        quant("f", T.ft, HC * h, HC * h + HC, ["ft%d%d" % (h, b) for b in range(4)], ["fq%d" % h])
+        send("f", "a", i, "fq%d" % h)
+    quant("v", T.vt, 0, 128, ["vt"], ["vq"])
+    keep("f", "a")
+    pick("vr", 0, 128, "v", 128, T.l_u[:, 0:8], ["vq", "l_u"], "vr")
+    op("v", lambda: V.memset(T.half[:], 0.5), [], ["half"])
+    quant("e", T.et, 0, 512, ["et%d" % b for b in range(4)], ["eq_"])
+    store_order(0, "oaf", T.oa)
+
+    for h in (early, late):
+        a, first = products("w", "a", h, range(4), ["wq", "ws"])
+        for b in range(4):
+            out, src, keys = elem(T.ht, b, a, a + HC), bank(first + b), (["ps%d" % (first + b)], ["ht%d%d" % (h, b)])
+            if b % 2:
+                op("v", lambda: V.tensor_scalar(out, src, 0.00390625, None, A.mult), *keys)
+            else:
+                op("s", lambda: SC.activation(out, src, F.Identity, scale=0.00390625), *keys)
+        quant("h", T.ht, a, a + HC, ["ht%d%d" % (h, b) for b in range(4)], ["hq%d" % h])
+    for h in (early, late):
+        scores("vr", "h", h, h == late, ["vrq", "vrs", "hq%d" % h])
+    rank_columns("place2", "order2", 1)
+    for b in (0, 1, 3, 2):
+        move("s", plane(T.hp, b), elem(T.ht, b), ["ht0%d" % b, "ht1%d" % b], ["hp%d" % b])
+
+    def sort_h(q, b):
+        move(q, plane(T.hs, b), plane(T.hp, b).indirect(T.order2[:, 0:KB]), ["hp%d" % b, "order2"], ["hs%d" % b])
+
+    def scan(b):
+        op("v", lambda: V.tensor_tensor_scan(plane(T.rs, b), T.half[:], plane(T.hs, b), 0.0, A.mult, A.max), ["half", "hs%d" % b], ["rs%d" % b])
+
+    def back(q, b, h, a=0, z=HB):
+        key = "tt%d%d%d" % (h, b, a)
+        gather(q, T.tt, T.rs, b, "place2", HB * h + a, HB * h + z, ["rs%d" % b, "place2v", "place2s"], key)
+        return key
+
+    sort_h("v", 0)
+    sort_h("s", 1)
+    sort_h("s", 3)
+    scan(0)
+    scan(1)
+    keys = [back("s", 0, early), back("s", 1, early)]
+    sort_h("v", 2)
+    scan(3)
+    scan(2)
+    keys += [back("s", 3, early), back("v", 2, early)]
+    quant("t", T.tt, HC * early, HC * early + HC, keys, ["tq%d" % early])
+    send("t", "b", 0, "tq%d" % early)
+    keys = [back("s", 0, late), back("s", 1, late), back("v", 2, late), back("s", 3, late, 0, 8), back("v", 3, late, 8, HB)]
+    quant("t", T.tt, HC * late, HC * late + HC, keys, ["tq%d" % late])
+    send("t", "b", 1, "tq%d" % late)
+    keep("t", "b")
+    quant("m", T.mt, 0, 128, ["mt"], ["mq"])
+    store_order(1, "obf", T.ob)
+
+    for h in (early, late):
+        a, first = products("e", "b", h, (0, 2, 1, 3), ["eq_"])
+        for b in (0, 1):
+            op("v", lambda: V.tensor_tensor(plane(T.zs, b, a, a + HC), bank(first + b), elem(T.ft, b, a, a + HC), A.add),
+               ["ps%d" % (first + b), "ft%d%d" % (h, b)], ["zs%d%d" % (h, b)])
+        for b in (2, 3):
+            move("s", plane(T.zs, b, a, a + HC), bank(first + b), ["ps%d" % (first + b)], ["zs%d%d" % (h, b)])
+
+    def store_y(i):
+        a, z = 16 * ZP[i], 16 * ZP[i + 1]
+        q, dq = ("v", "y") if i == len(ZP) - 2 else ("s", "s")
+        move(q, T.yf[:, a:z], bank(4 + i, 0, z - a), ["ps%d" % (4 + i)], ["y%d" % i])
+        op(dq, lambda: Q[dq].dma_start(T.y[:, a:z], T.yf[:, a:z]), ["y%d" % i], out=True)
+
+    for i in range(len(ZP) - 1):
+        a, z = ZP[i], ZP[i + 1]
+        for b in range(4):
+            reads = ["zs0%d" % b, "zs1%d" % b, "place1v", "place1s"]
+            if b < 2:
+                gather("s", T.zt, T.zs, b, "place1", a, z, reads, "zt%d%d" % (i, b))
+            else:
+                op("v", lambda: V.tensor_tensor(elem(T.zt, b, 16 * a, 16 * z), plane(T.zs, b).indirect(T.place1[:, a:z]),
+                                                elem(T.xt, b, 16 * a, 16 * z), A.add), reads, ["zt%d%d" % (i, b)])
+        quant("z", T.zt, 16 * a, 16 * z, ["zt%d%d" % (i, b) for b in range(4)], ["zq%d" % i])
+        mm(4 + i, "m", 0, "z", 16 * a, 16 * z, ["mq", "zq%d" % i])
+        op("y", lambda: g.sync.dma_start(T.oc[:, 64 * a:64 * z], u8(T.z_q[:, 16 * a:16 * z])), ["zq%d" % i], out=True)
+        if i:
+            store_y(i - 1)
+    for k in range(4):
+        op("s", lambda: SC.dma_start(T.osc[4 * k:4 * k + 4, :], T.z_s[32 * k:32 * k + 4, :]), ["zq%d" % i for i in range(len(ZP) - 1)], out=True)
+    store_y(len(ZP) - 2)
+
+    g.wait_ge(T.sem.sent, total["sent"])
+    for s in sorted(last_on, key=lambda x: last_on[x]):
+        if waited.get(s, 0) < total[s]:
+            g.wait_ge(T.sem[s], total[s])
+    g.wait_ge(T.sem.outs, total["outs"])

@@ -3,43 +3,65 @@ from concourse.mybir import dt, AluOpType as A, ActivationFunctionType as F
 
 C, S, N = 448, 112, 4
 KB = C // 16
-KV = 12
-KS = KB - KV
-CV, CS = 16 * KV, 16 * KS
+KV = 8
+K0 = 18
+HM = K0 // 2
+KS, K1, K2 = KB - KV, K0 - KV, KB - K0
+CV, CS, C0, C2 = 16 * KV, 16 * KS, 16 * K0, 16 * K2
 HC, HB = C // 2, KB // 2
-ZP = [0, 14, 28]
+CP = C + 32
+WIN = 4 * C - 3
+LOW = 64
+ZP = [0, 18, 28]
 GS, GV = 4, 4
-X4, U8, BF, F32 = "float8_e4m3fn_x4", "uint8", "bfloat16", "float32"
+X4, U8, BF, F32, F16 = "float8_e4m3fn_x4", "uint8", "bfloat16", "float32", "float16"
+
+CUTS = [KV]
+_s = 0
+for _k in range(KV, KB):
+    if _s + 16 * min(_k, K0) > 2048:
+        CUTS.append(_k)
+        _s = 0
+    _s += 16 * min(_k, K0)
+CUTS.append(KB)
+NC = len(CUTS) - 1
+CW = HM * (1 + 16 * max(CUTS[_k + 1] - CUTS[_k] for _k in range(NC)))
+SG = [sum(C - 16 * (j + 1) for j in range(KV, k)) for k in range(KV, K0 + 1)]
 
 SCRATCH = {
-    "xt": ("sbuf", [128, 4 * C], BF), "ut": ("sbuf", [128, 512], BF), "vt": ("sbuf", [128, 512], BF), "mt": ("sbuf", [128, 512], BF),
-    "xp": ("sbuf", [128, 4 * C], BF), "ft": ("sbuf", [128, 4 * C], BF), "ht": ("sbuf", [128, 4 * C], BF), "hp": ("sbuf", [128, 4 * C], BF),
-    "hs": ("sbuf", [128, 4 * C], BF), "rs": ("sbuf", [128, 4 * C], BF), "tt": ("sbuf", [128, 4 * C], BF),
+    "xt": ("sbuf", [128, 4 * CP], BF), "ut": ("sbuf", [128, 512], BF), "vt": ("sbuf", [128, 512], BF), "mt": ("sbuf", [128, 512], BF),
+    "x1": ("sbuf", [128, 4 * C], BF), "x2": ("sbuf", [128, 4 * C], BF), "x3": ("sbuf", [128, 4 * C], BF),
+    "h1": ("sbuf", [128, 4 * C], BF), "h2": ("sbuf", [128, 4 * C], BF), "h3": ("sbuf", [128, 4 * C], BF),
+    "ft0": ("sbuf", [128, 2 * C], BF), "ft1": ("sbuf", [128, 512], BF), "ft2": ("sbuf", [128, 512], BF),
+    "tt0": ("sbuf", [128, 2 * C], BF), "tt1": ("sbuf", [128, 512], BF), "tt2": ("sbuf", [128, 512], BF),
+    "ht": ("sbuf", [128, 4 * CP], BF), "hs": ("sbuf", [128, 4 * C], BF), "rs": ("sbuf", [128, 4 * C], BF),
     "zs": ("sbuf", [128, 4 * C], BF), "zt": ("sbuf", [128, 4 * C], BF),
     "ones": ("sbuf", [128, 512], BF), "et": ("sbuf", [128, 2048], BF),
-    "sp": ("sbuf", [128, C + 16], F32), "turn": ("sbuf", [128, 928], F32), "dpos": ("sbuf", [128, 32], F32), "dneg": ("sbuf", [128, 32], F32),
+    "sp": ("sbuf", [128, C], F32), "turn": ("sbuf", [128, C + CP], F32), "dpos": ("sbuf", [128, 32], F32), "dneg": ("sbuf", [128, 32], F32),
     "eq": ("sbuf", [128, C], BF), "eqs": ("sbuf", [128, C], BF), "after": ("sbuf", [128, C], BF), "cidx": ("sbuf", [128, C], BF),
+    "lt": ("sbuf", [128, CS], BF), "lts": ("sbuf", [128, CS], BF), "cap1": ("sbuf", [128, CS], BF),
     "vals": ("sbuf", [128, C], BF), "half": ("sbuf", [128, C], BF),
-    "cst": ("sbuf", [128, KB], F32), "cc": ("sbuf", [128, KB], BF),
-    "mask": ("sbuf", [128, KV * C], BF), "sgn": ("sbuf", [128, KS * CS], BF), "sums": ("sbuf", [128, KV * HC], BF),
-    "cols": ("sbuf", [128, KV * (CS + 32)], BF), "colt": ("sbuf", [128, 2 * CS + 32], BF), "colu": ("sbuf", [128, 2 * CS + 32], BF),
-    "cap1": ("sbuf", [128, KV * CS], BF), "cap2": ("sbuf", [128, 2 * CS + 32], BF),
-    "acc": ("sbuf", [128, 3 * KS], F32), "acce": ("sbuf", [128, 3 * KS], F32), "turns": ("sbuf", [128, 3 * KS + 3], F32),
-    "inv": ("sbuf", [128, 960], BF), "invt": ("sbuf", [128, 928], BF),
+    "cst": ("sbuf", [128, KV], F32), "cc": ("sbuf", [128, KV], BF),
+    "ma": ("sbuf", [128, HM * C], BF), "mb": ("sbuf", [128, HM * CS], BF),
+    "sgn": ("sbuf", [128, SG[-1]], BF), "sg2": ("sbuf", [128, K2 * C2], BF), "sums": ("sbuf", [128, KV * HC], BF),
+    "cum": ("sbuf", [128, NC * CW], F16), "cols": ("sbuf", [128, CS + 32], BF),
+    "colt": ("sbuf", [128, 2 * CS + 32], BF), "colu": ("sbuf", [128, 2 * CS + 32], BF), "cap2": ("sbuf", [128, 2 * CS + 32], BF),
+    "acc": ("sbuf", [128, 96], F32), "acce": ("sbuf", [128, 96], F32), "turns": ("sbuf", [128, 99], F32), "pl": ("sbuf", [128, 32], F32),
+    "inv": ("sbuf", [128, 2 * CP], BF), "invt": ("sbuf", [128, C + CP], BF),
     "oaf": ("sbuf", [128, C], F32), "obf": ("sbuf", [128, C], F32), "yf": ("sbuf", [128, C], F32),
-    "i16": ("sbuf", [128, KB], "int32"), "cx": ("sbuf", [128, 128], F32), "cxt": ("sbuf", [128, 128], F32),
-    "l_u": ("sbuf", [128, 8], "uint16"), "l_d": ("sbuf", [128, 4], "uint16"), "l_rep": ("sbuf", [128, KB], "uint16"),
-    "l_own": ("sbuf", [128, 8], "uint16"), "l_col": ("sbuf", [128, 2], "uint16"),
+    "i16": ("sbuf", [128, 8], "int32"), "cx": ("sbuf", [128, 128], F32), "cxt": ("sbuf", [128, 128], F32),
+    "l_u": ("sbuf", [128, 8], "uint16"), "l_d": ("sbuf", [128, 2], "uint16"), "l_rep": ("sbuf", [128, 32], "uint16"),
+    "l_col": ("sbuf", [128, 2], "uint16"), "l_p": ("sbuf", [128, 2], "uint16"),
     "place1": ("sbuf", [128, KB], "uint16"), "place2": ("sbuf", [128, KB], "uint16"),
     "order1": ("sbuf", [128, 32], "uint16"), "order2": ("sbuf", [128, 32], "uint16"),
     "ps": ("psum", [128, 4096], F32),
 }
-for _n, _w in (("x", C), ("u", 128), ("ur", 128), ("v", 128), ("vr", 128), ("m", 128), ("w", 512), ("e", 512),
-               ("f", C), ("a", C), ("h", C), ("t", C), ("b", C), ("z", C)):
+for _n, _w in (("x", CP), ("u", 128), ("ur", 128), ("v", 128), ("vr", 128), ("m", 128), ("w", 512), ("e", 512),
+               ("f0", HC), ("f1", 128), ("f2", 128), ("a", 3 * S), ("h", CP), ("t0", HC), ("t1", 128), ("t2", 128), ("b", 3 * S), ("z", C)):
     SCRATCH[_n + "_q"] = ("sbuf", [128, _w], X4)
     SCRATCH[_n + "_s"] = ("sbuf", [128, _w], U8)
 
-POOL = ["e%d" % i for i in range(110)]
+POOL = ["e%d" % i for i in range(130)]
 LOADS = ["ld%d" % i for i in range(8)]
 SEMAPHORES = POOL + LOADS + ["far_a", "near_a", "far_b", "near_b", "sent", "outs"]
 
@@ -61,23 +83,27 @@ def rank_program(g, core, T, topo):
     V, SC, PE = g.vector, g.scalar, g.tensor
     late = rank // 2
     early = 1 - late
+    mate = 2 * late + 1 - rank % 2
+    PIECE = [(HB * early, HB, 0, HC), (HB * late + 6 * (mate % 2), 8, 16 * (mate % 2), S), (HB * late + 6 * (rank % 2), 8, 16 * (rank % 2), S)]
 
     known = {q: set() for q in Q}
     events = []
-    total, last_on, waited = {}, {}, {}
+    total, last_on, waited, tags = {}, {}, {}, {}
     writer, readers = {}, {}
+    closed = set()
     loads = list(LOADS)
 
     def wait(q, e):
-        if e in known[q]:
+        if e is None or e in known[q]:
             return
-        s, n, k = events[e]
+        s, n, k = events[e][0:3]
+        closed.add(e)
         Q[q].wait_ge(T.sem[s], n)
         waited[s] = max(waited.get(s, 0), n)
         known[q].add(e)
         known[q].update(k)
 
-    def op(q, make, reads=(), writes=(), join=None, load=False, out=False):
+    def op(q, make, reads=(), writes=(), tag=None, on=None, load=False, out=False):
         need = set()
         for k in reads:
             if k in writer:
@@ -88,26 +114,28 @@ def rank_program(g, core, T, topo):
             if k in writer:
                 need.add(writer[k])
             need.update(e for e, qq in readers.get(k, []))
-        need.discard(join)
-        for e in sorted(need, reverse=True):
-            wait(q, e)
+        e = tags.get(tag)
+        assert e is None or (e not in need and e not in closed), tag
+        for x in sorted(need, reverse=True):
+            wait(q, x)
         if out:
             make().then_inc(T.sem.outs, 16)
             total["outs"] = total.get("outs", 0) + 16
-            return None
+            return
         step = 16 if load else 1
-        if join is None:
+        if e is None:
             if load:
                 s = loads.pop(0)
             else:
-                free = [x for x in POOL if x in last_on and last_on[x] in known[q]]
+                free = [x for x in POOL if x in last_on and all(last_on[x] in known[y] for y in (on or q))]
                 s = min(free, key=lambda x: last_on[x]) if free else [x for x in POOL if x not in last_on][0]
             e = len(events)
-            events.append([s, 0, set()])
+            events.append([s, 0, set(), last_on.get(s)])
             last_on[s] = e
-        else:
-            e = join
-            s = events[e][0]
+            if tag is not None:
+                tags[tag] = e
+        s = events[e][0]
+        assert events[e][3] is None or events[e][3] in known[q], tag
         make().then_inc(T.sem[s], step)
         total[s] = total.get(s, 0) + step
         events[e][1] = total[s]
@@ -117,7 +145,6 @@ def rank_program(g, core, T, topo):
         for k in writes:
             writer[k] = e
             readers[k] = []
-        return e
 
     def bank(i, a=0, b=HC):
         return T.ps[:, 512 * i + a:512 * i + b]
@@ -128,24 +155,26 @@ def rank_program(g, core, T, topo):
     def u32(ap):
         return ap.bitcast(dt.uint32)
 
-    def quant(name, src, a, b, reads, writes):
-        return op("v", lambda: V.quantize_mx(T[name + "_q"][:, a:b], T[name + "_s"][:, a:b], src[:, 4 * a:4 * b]), reads, writes)
+    def quant(name, src, a, b, reads, writes, tag=None):
+        op("v", lambda: V.quantize_mx(T[name + "_q"][:, a:b], T[name + "_s"][:, a:b], src[:, 4 * a:4 * b]), reads, writes, tag)
 
-    def mm(i, w, wa, x, a, b, reads):
-        return op("t", lambda: PE.matmul_mx(bank(i, 0, b - a), T[w + "_q"][:, wa:wa + 128], T[w + "_s"][:, wa:wa + 128],
-                                            T[x + "_q"][:, a:b], T[x + "_s"][:, a:b], True, True), reads, ["ps%d" % i])
+    def mm(i, w, wa, x, a, b, reads, tag=None):
+        op("t", lambda: PE.matmul_mx(bank(i, 0, b - a), T[w + "_q"][:, wa:wa + 128], T[w + "_s"][:, wa:wa + 128],
+                                     T[x + "_q"][:, a:b], T[x + "_s"][:, a:b], True, True), reads, ["ps%d" % i], tag)
 
-    def pick(dst, a, b, src, width, lst, reads, key):
-        op("v", lambda: V.tensor_copy(u32(T[dst + "_q"][:, a:b]), u32(T[src + "_q"][:, 0:width]).indirect(lst)), reads, [key + "q"])
-        op("s", lambda: SC.activation(T[dst + "_s"][:, a:b], T[src + "_s"][:, 0:width].indirect(lst), F.Copy), reads, [key + "s"])
+    def pick(dst, src):
+        lst, reads = T.l_u[:, 0:8], [src + "q", "l_u"]
+        op("v", lambda: V.tensor_copy(u32(T[dst + "_q"][:]), u32(T[src + "_q"][:]).indirect(lst)), reads, [dst + "q"], dst, "vs")
+        op("s", lambda: SC.activation(T[dst + "_s"][:], T[src + "_s"][:].indirect(lst), F.Copy), reads, [dst + "s"], dst, "vs")
 
-    def move(q, out, in_, reads, writes):
+    def move(q, out, in_, reads, writes, tag=None, on=None):
         if q == "v":
-            return op("v", lambda: V.tensor_copy(out, in_), reads, writes)
-        return op("s", lambda: SC.activation(out, in_, F.Copy), reads, writes)
+            op("v", lambda: V.tensor_copy(out, in_), reads, writes, tag, on)
+        else:
+            op("s", lambda: SC.activation(out, in_, F.Copy), reads, writes, tag, on)
 
-    def turn(out, in_, reads, writes, join=None):
-        return op("v", lambda: V.transpose(out, in_), reads, writes, join=join)
+    def turn(out, in_, reads, writes, tag=None):
+        op("v", lambda: V.transpose(out, in_), reads, writes, tag)
 
     def elem(t, b, a=0, z=C):
         return t[:, 4 * a + b:4 * z:4]
@@ -153,254 +182,339 @@ def rank_program(g, core, T, topo):
     def plane(t, b, a=0, z=C):
         return t[:, C * b + a:C * b + z]
 
-    def gather(q, dst, src, b, lst, a, z, reads, key):
-        move(q, elem(dst, b, 16 * a, 16 * z), plane(src, b).indirect(T[lst][:, a:z]), reads, [key])
-
     op("s", lambda: SC.dma_start(T.ut[:], T.u[:]), [], ["ut"], load=True)
-    op("y", lambda: g.sync.dma_start(T.xt[:, 0:2 * C], T.x[:, 0:2 * C]), [], ["xt0"], load=True)
-    op("y", lambda: g.sync.dma_start(T.xt[:, 2 * C:4 * C], T.x[:, 2 * C:4 * C]), [], ["xt1"], load=True)
+    op("y", lambda: g.sync.dma_start(T.xt[:, 64:64 + 2 * C], T.x[:, 0:2 * C]), [], ["xt0"], load=True)
+    op("y", lambda: g.sync.dma_start(T.xt[:, 64 + 2 * C:64 + 4 * C], T.x[:, 2 * C:4 * C]), [], ["xt1"], load=True)
     XT = ["xt0", "xt1"]
-    op("y", lambda: g.sync.dma_start(T.vt[:], T.v[:]), XT, ["vt"], load=True)
-    op("y", lambda: g.sync.dma_start(u8(T.w_q[:]), T.wc[:]), [], ["wq"], load=True)
-    op("y", lambda: g.sync.dma_start(T.w_s[:], T.ws[:]), [], ["ws"], load=True)
-    op("y", lambda: g.sync.dma_start(T.mt[:], T.m[:]), [], ["mt"], load=True)
+    op("y", lambda: g.sync.dma_start(T.vt[:], T.v[:]), XT, ["vt"], "more", load=True)
+    for b in (1, 2, 3):
+        op("y", lambda: g.sync.dma_start(T["x%d" % b][:, 0:WIN], T.x[:, b:b + WIN]), [], ["x%d" % b], "more", load=True)
+    op("y", lambda: g.sync.dma_start(u8(T.w_q[:]), T.wc[:]), [], ["wq"], "more", load=True)
+    op("y", lambda: g.sync.dma_start(T.w_s[:], T.ws[:]), [], ["ws"], "more", load=True)
+    op("y", lambda: g.sync.dma_start(T.mt[:], T.m[:]), [], ["mt"], "more", load=True)
 
-    def iota(out, pattern, base, key):
-        op("g", lambda: g.iota(out, pattern, base, 0, allow_small_or_imprecise_dtypes=True), [], [key])
+    def iota(out, pattern, base, keys, tag):
+        op("g", lambda: g.iota(out, pattern, base, 0, allow_small_or_imprecise_dtypes=True), [], keys, tag)
 
-    op("g", lambda: g.iota(T.i16[:], [[16, KB]], 0, 0), [], ["i16"])
-    for a, far, base in ((0, C + 16, 0), (32, C + 16, 0), (96, CS + 16, 15)):
-        iota(T.cx[:, a:a + 16], [[32, 8], [16 + far, 2]], base, "cx%da" % a)
-        iota(T.cx[:, a + 16:a + 32], [[32, 8], [16 - far, 2]], base + far, "cx%db" % a)
-    iota(T.cx[:, 64:96], [[0, 2], [1, 16]], 0, "cx64")
-    iota(T.cidx[:], [[0, KB], [1, 16]], 0, "cidx")
-    iota(T.vals[:], [[1, C]], -HC, "vals")
-    iota(T.turns[:], [[0, KS + 1], [1, 3]], -1, "turns")
-    iota(T.cap1[:], [[0, CS], [1, KV]], 0, "cap1")
-    iota(T.cap2[:], [[0, 2 * KS + 2], [KV, 16]], 0, "cap2")
+    def zero(out, n, keys, tag):
+        iota(out, [[0, n]], 0, keys, tag)
 
-    op("v", lambda: V.memset(T.turn[:, 448:480], 0.0), [], ["turnpad"])
-    op("v", lambda: V.memset(T.acc[:], 0.0), [], ["accu%d" % k for k in range(KS)] + ["accl%d" % k for k in range(KS)] + ["accc"])
-    op("v", lambda: V.memset(T.cst[:, 0:KV], -HC - 1.0), [], ["cstv"])
-    op("v", lambda: V.memset(T.inv[:], 0.0), [], ["inv0", "inv1"])
-    op("v", lambda: V.memset(T.cols[:, 0:CV], 0.0), [], ["colpad0"])
-    op("v", lambda: V.memset(T.cols[:, CV + KV * CS:2 * CV + KV * CS], 0.0), [], ["colpad1"])
-    op("v", lambda: V.memset(T.ones[:], 1.0), [], ["ones"])
-    op("v", lambda: V.tensor_copy(T.l_u[:], T.i16[:, 0:8]), ["i16"], ["l_u"])
-    op("v", lambda: V.tensor_scalar(T.l_rep[:], T.i16[:], 0.0625, None, A.mult), ["i16"], ["l_rep"])
-    op("v", lambda: V.tensor_scalar(T.cst[:, KV:KB], T.i16[:, KV:KB], 15.0 - HC, None, A.add), ["i16"], ["csts"])
-    op("v", lambda: V.memset(T.cx[:, 16:17], 912.0), [], ["cx0b"])
-    turn(T.cxt[:], T.cx[:], ["cx0a", "cx0b", "cx32a", "cx32b", "cx96a", "cx96b", "cx64"], ["cxt"])
-    op("v", lambda: V.tensor_copy(T.l_d[:, 0:3:2], T.cxt[:, 0:33:32]), ["cxt"], ["l_d0"])
-    op("v", lambda: V.tensor_scalar(T.l_d[:, 1:4:2], T.cxt[:, 32:34], 256.0, 927.0, A.add, A.min), ["cxt"], ["l_d1"])
-    op("v", lambda: V.tensor_copy(T.l_col[:], T.cxt[:, 96:98]), ["cxt"], ["l_col"])
-    op("v", lambda: V.tensor_scalar(T.l_own[:, 0:7], T.i16[:, 0:7], T.cxt[:, 64:65], float(S * rank), A.add, A.add), ["i16", "cxt"], ["l_own"])
+    for a, far, base in ((0, C + 16, 0), (64, CS + 16, 15)):
+        iota(T.cx[:, a:a + 16], [[32, 8], [16 + far, 2]], base, ["cx%da" % a], "cx")
+        iota(T.cx[:, a + 16:a + 32], [[32, 8], [16 - far, 2]], base + far, ["cx%db" % a], "cx")
+    iota(T.cx[:, 32:64], [[0, 2], [1, 16]], 0, ["cx32"], "cx")
+    iota(T.cx[:, 96:128], [[1, 32]], 0, ["cx96"], "cx")
+    op("g", lambda: g.iota(T.i16[:], [[16, 8]], 0, 0), [], ["i16"])
+    iota(T.cidx[:], [[0, KB], [1, 16]], 0, ["cidx"], None)
+    zero(T.lt[:, C0 - CV:CS], C2, ["ltpad"], "g1")
+    iota(T.cap1[:], [[-16, KS], [1, 16]], HC + LOW - 15 - CV, ["cap1"], "g1")
+    iota(T.cst[:], [[0, KV]], -HC - 1, ["cst"], "g1")
+    zero(T.ma[:, HM * CV:HM * 16 * HM], HM * (16 * HM - CV), ["mu%d" % k for k in range(HM)], "g1")
+    zero(T.acc[:], 96, ["acc%d" % k for k in range(96)], "g1")
+    zero(T.mb[:, 0:HM * (C0 - CV)], HM * (C0 - CV), ["mu%d" % k for k in range(HM, K0)], None)
+    iota(T.vals[:], [[1, C]], -HC, ["vals"], "g2")
+    iota(T.turns[:], [[0, 33], [1, 3]], -1, ["turns"], "g2")
+    iota(T.cap2[:], [[0, 2 * KS + 2], [32, 16]], -LOW, ["cap2"], "g2")
+    zero(T.cols[:, 0:16], 16, ["colpad0"], "g2")
+    zero(T.cols[:, CS + 16:CS + 32], 16, ["colpad1"], "g2")
+    zero(T.inv[:], 2 * CP, ["inv0", "inv1"], "g2")
+    iota(T.ones[:], [[0, 512]], 1, ["ones"], None)
     for b in range(4):
         op("g", lambda b=b: g.affine_select(T.et[:, 512 * b:512 * b + 512], T.ones[:], [[1, 512]], A.is_equal, 0.0, -b, -4),
-           ["ones"], ["et%d" % b])
+           ["ones"], ["et%d" % b], "et")
 
-    def scores(w, x, h, last, reads):
+    for t in ("xt", "ht"):
+        op("v", lambda: V.memset(T[t][:, 0:64], 0.0), [], [t + "pad0"], "v0")
+        op("v", lambda: V.memset(T[t][:, 4 * CP - 64:4 * CP], 0.0), [], [t + "pad1"], "v0")
+    op("v", lambda: V.memset(T.half[:], 0.5), [], ["half"], "v0")
+    op("v", lambda: V.memset(T.cum[:, HM - 1:NC * CW:CW], 0.0), [], ["cumpad"], "v0")
+    turn(T.cxt[:], T.cx[:], ["cx0a", "cx0b", "cx32", "cx64a", "cx64b", "cx96"], ["cxt"])
+    op("v", lambda: V.tensor_copy(T.l_u[:], T.i16[:]), ["i16"], ["l_u"], "uq")
+    op("v", lambda: V.tensor_copy(T.l_p[:, 0:1], T.cxt[:, 96:97]), ["cxt"], ["l_p"], "uq")
+    for name, a, top in (("l_d", 0, C + CP - 1), ("l_col", 64, 2 * CS + 31)):
+        op("v", lambda: V.tensor_copy(T[name][:, 0:1], T.cxt[:, a:a + 1]), ["cxt"], [name + "0"], "v1")
+        op("v", lambda: V.tensor_scalar(T[name][:, 1:2], T.cxt[:, a:a + 1], 256.0, float(top), A.add, A.min), ["cxt"], [name + "1"], "v1")
+
+    def lists():
+        src = T.cx[:, 0:32].indirect(T.l_p[:, 0:1])
+        op("v", lambda: V.tensor_copy(T.l_rep[:, 0:16], src), ["l_p"], ["l_rep0"], "v1")
+        op("v", lambda: V.tensor_scalar(T.l_rep[:, 16:32], src, 256.0, C + CP - 1.0, A.add, A.min), ["l_p"], ["l_rep1"], "v1")
+        op("v", lambda: V.tensor_scalar(T.after[:], T.cidx[:], T.cxt[:, 32:33], None, A.is_gt), ["cidx", "cxt"], ["after"], "v1")
+
+    def pack_half(name, h, reads):
+        a = CP // 2 * h
+        quant(name, T[name + "t"], a, a + CP // 2, reads + [name + "tpad%d" % h], [name + "q%d" % h])
+
+    def scores(w, x, h, last, slot):
         a, i = HC * h, 6 if last else 4
-        mm(i, w, 0, x, a, a + HC, reads)
-        mm(i + 1, w, 0, x, a, a + HC, reads)
-        if h == 0:
-            move("s", T.sp[:, C:C + 16], bank(i + 1, 0, 16), ["ps%d" % (i + 1)], ["spx"])
-        move("s", T.sp[:, a:a + HC], bank(i + 1), ["ps%d" % (i + 1)], ["sp%d" % h])
-        e = turn(T.turn[:, a:a + HC], bank(i), ["ps%d" % i], ["turna%d" % h])
-        turn(T.turn[:, 480 + a:672 + a], bank(i, 16, 208), ["ps%d" % i], ["turnb%d" % h], join=e)
-        if last:
-            turn(T.turn[:, 896:928], T.sp[:, 432:464], ["sp1", "spx"], ["turnd"], join=e)
-            turn(T.turn[:, 672:704], T.sp[:, 208:240], ["sp0", "sp1"], ["turnc"], join=e)
+        lo = h * (HC if last else HC + 16)
+        hi = CP if h else HC + (32 if last else 16)
+        s0, s1 = (lo if last else lo + 16 * h), (hi if last or h else hi - 16)
+        tn, sp, reads = "turn%d" % slot, "sp%d" % slot, [w + "q", w + "s", x + "q%d" % h]
+        mm(i, w, 0, x, lo, hi, reads + ([x + "q%d" % (1 - h)] if last else []))
+        mm(i + 1, w, 0, x, a + 16, a + 16 + HC, reads)
+        move("s", T.sp[:, a:a + HC], bank(i + 1), ["ps%d" % (i + 1)], ["sp%d" % h], sp)
+        turn(T.turn[:, a:a + HC], bank(i, a + 16 - lo, a + 16 - lo + HC), ["ps%d" % i], ["turna%d" % h], tn)
+        turn(T.turn[:, C + s0:C + s1], bank(i, s0 - lo, s1 - lo), ["ps%d" % i], ["turnb%d" % h], tn)
 
     def rank_columns(place, order, slot):
-        turned = ["turna0", "turna1", "turnb0", "turnb1", "turnc", "turnd", "turnpad", "l_d0", "l_d1"]
+        turned = ["turna0", "turna1", "turnb0", "turnb1", "l_d0", "l_d1", "l_rep0", "l_rep1"]
         SP = ["sp0", "sp1"]
-        one = {}
 
-        def joined(name, q, make, reads, writes):
-            one[name] = op(q, make, reads, writes, join=one.get(name))
-
-        op("s", lambda: SC.activation(T.dneg[:], T.turn[:, 0:928].indirect(T.l_d[:, 0:2]), F.Identity, scale=-1.0), turned, ["dneg"])
-        move("v", T.dpos[:], T.turn[:, 0:928].indirect(T.l_d[:, 0:2]), turned, ["dpos"])
-
-        def sign(k):
-            joined(("sign", k // GS), "s",
-                   lambda: SC.activation(T.sgn[:, CS * k:CS * k + CS], T.sp[:, CV:C], F.Sign, bias=T.dneg[:, KV + k:KV + k + 1]),
-                   SP + ["dneg"], ["sgl%d" % k, "sgu%d" % k])
-
-        def count(k):
-            a, n = CS * k, 16 * k + 16
-            lo, up = T.sgn[:, a:a + n], T.sgn[:, a + n:a + CS]
-            joined("count", "s", lambda: SC.activation(lo, lo, F.Relu, scale=-1.0, accum_out=T.acc[:, 3 * k + 1:3 * k + 2]),
-                   [], ["sgl%d" % k, "accl%d" % k])
-            if n < CS:
-                joined("count", "s", lambda: SC.activation(up, up, F.Relu, accum_out=T.acc[:, 3 * k + 2:3 * k + 3]),
-                       [], ["sgu%d" % k, "accu%d" % k])
-
-        for k in range(KS + GS + 1):
-            if k < KS:
-                sign(k)
-            if k > GS:
-                count(k - GS - 1)
+        def one(q, make, reads, writes, tag=None):
+            op(q, make, reads, writes, None if tag is None else (slot, tag))
 
         def row(k, a, z):
-            return T.mask[:, KV * a + k:KV * z:KV]
+            if k < HM:
+                return T.ma[:, HM * a + k:HM * z:HM]
+            return T.mb[:, HM * (a - CV) + k - HM:HM * (z - CV):HM]
+
+        def acc(k, j):
+            i = 3 * (k - KV) + j
+            return T.acc[:, i:i + 1], "acc%d" % i
+
+        one("s", lambda: SC.activation(T.dneg[:], T.turn[:].indirect(T.l_d[:]), F.Identity, scale=-1.0), turned, ["dneg"])
+        move("v", T.dpos[:], T.turn[:].indirect(T.l_d[:]), turned, ["dpos"])
+
+        def sign(k):
+            if k < K0:
+                out, a = T.sgn[:, SG[k - KV]:SG[k - KV + 1]], 16 * k + 16
+            else:
+                out, a = T.sg2[:, C2 * (k - K0):C2 * (k - K0 + 1)], C0
+            one("s", lambda: SC.activation(out, T.sp[:, a:C], F.Sign, bias=T.dneg[:, k:k + 1]),
+                SP + ["dneg"], ["sgl%d" % k, "sgu%d" % k], ("sign", (k - KV) // GS))
+
+        def count(k):
+            (lo_sum, lo_key), (up_sum, up_key) = acc(k, 1), acc(k, 2)
+            if k < K0:
+                one("s", lambda: SC.activation(row(k, 16 * k + 16, C), T.sgn[:, SG[k - KV]:SG[k - KV + 1]], F.Relu, accum_out=up_sum),
+                    ["sgu%d" % k], ["mu%d" % k, up_key], ("up", k < max(HM, CUTS[1] - 1)))
+                return
+            a, n = C2 * (k - K0), 16 * (k - K0) + 16
+            lo, up = T.sg2[:, a:a + n], T.sg2[:, a + n:a + C2]
+            one("s", lambda: SC.activation(lo, lo, F.Relu, scale=-1.0, accum_out=lo_sum), [], ["sgl%d" % k, lo_key], "count")
+            if n < C2:
+                one("s", lambda: SC.activation(up, up, F.Relu, accum_out=up_sum), [], ["sgu%d" % k, up_key], "count")
+
+        starts = list(range(KV, KB, GS))
+        for i in range(len(starts) + 1):
+            for k in range(KV + GS * i, min(KB, KV + GS * i + GS)):
+                sign(k)
+            if i:
+                for k in range(starts[i - 1], min(KB, starts[i - 1] + GS)):
+                    count(k)
 
         def compare(k):
             n = 16 * k + 16
             for a, z, how, name in ((0, n, A.is_ge, "ml%d"), (n, C, A.is_gt, "mu%d")):
-                joined(("mask", k // GV), "v", lambda: V.tensor_scalar(row(k, a, z), T.sp[:, a:z], T.dpos[:, k:k + 1], None, how),
-                       SP + ["dpos"], [name % k])
+                one("v", lambda: V.tensor_scalar(row(k, a, z), T.sp[:, a:z], T.dpos[:, k:k + 1], None, how),
+                    SP + ["dpos"], [name % k], ("mask", k // GV))
 
         def add_up(k):
-            joined("sum", "v", lambda: V.tensor_tensor_scan(T.sums[:, HC * k:HC * k + HC], row(k, 0, HC), row(k, HC, C), T.cc[:, k:k + 1],
-                                                            A.add, A.add), ["ml%d" % k, "mu%d" % k, "cc"], ["sum%d" % k])
+            one("v", lambda: V.tensor_tensor_scan(T.sums[:, HC * k:HC * k + HC], row(k, 0, HC), row(k, HC, C), T.cc[:, k:k + 1], A.add, A.add),
+                ["ml%d" % k, "mu%d" % k, "cc"], ["sum%d" % k], "sum")
 
-        o = 480 * slot
+        def run_up(i):
+            a, z = 16 * CUTS[i], 16 * CUTS[i + 1]
+            o = CW * i + HM
+            one("v", lambda: V.tensor_tensor_scan(T.cum[:, o:o + HM * (z - a)], T.ma[:, HM * a:HM * z], T.mb[:, HM * (a - CV):HM * (z - CV)],
+                                                  0.0, A.add, A.add), ["mu%d" % k for k in range(K0) if k < max(HM, CUTS[i + 1] - 1)], ["cum%d" % i], "cum")
+
+        def differ(i):
+            a, z = 16 * CUTS[i], 16 * CUTS[i + 1]
+            o = CW * i + HM - 1
+            n = HM * (z - a)
+            one("v", lambda: V.tensor_tensor_scan(T.cols[:, 16 + a - CV:16 + z - CV], T.cum[:, o + HM:o + n + 1:HM], T.cum[:, o:o + n:HM],
+                                                  0.0, A.max, A.subtract), ["cum%d" % i, "cumpad"], ["cols%d" % i], "cols")
+
+        o = CP * slot
         key = "inv%d" % slot
 
         def scatter(a, z, part):
-            op("v", lambda: V.tensor_copy(T.inv[:, o + 16:o + 16 + C].indirect(T[place][:, a:z]), T.vals[:, 16 * a:16 * z]), [part, "vals"], [key])
+            one("v", lambda: V.tensor_copy(T.inv[:, o + 16:o + 16 + C].indirect(T[place][:, a:z]), T.vals[:, 16 * a:16 * z]), [part, "vals"], [key])
 
-        op("v", lambda: V.tensor_tensor(T.eq[:], T.dpos[:, 0:32].indirect(T.l_rep[:, 0:KB]), T.sp[:, 0:C], A.is_equal),
-           SP + ["dpos", "l_rep"], ["eq"])
+        one("v", lambda: V.tensor_tensor(T.eq[:], T.turn[:].indirect(T.l_rep[:, 0:KB]), T.sp[:], A.is_equal), SP + turned, ["eq"], "eq")
+        one("v", lambda: V.tensor_tensor(T.lt[:, 0:C0 - CV], T.turn[:].indirect(T.l_rep[:, KV:K0]), T.sp[:, CV:C0], A.is_gt), SP + turned, ["lt"], "eq")
         compare(0)
-        op("v", lambda: V.tensor_tensor_scan(T.eqs[:], T.eq[:], T.after[:], 0.0, A.add, A.mult), ["eq", "after"], ["eqs"])
+        one("v", lambda: V.tensor_tensor_scan(T.eqs[:], T.eq[:], T.after[:], 0.0, A.add, A.mult), ["eq", "after"], ["eqs"], "eqs")
+        one("v", lambda: V.tensor_tensor_scan(T.lts[:], T.cap1[:], T.lt[:], 0.0 + HC + LOW, A.min, A.add), ["lt", "ltpad", "cap1"], ["lts"], "eqs")
         compare(1)
-        op("v", lambda: V.tensor_tensor(T.cc[:], T.cst[:], T.eqs[:, 15:C:16], A.subtract), ["cstv", "csts", "eqs"], ["cc"])
+        one("v", lambda: V.tensor_tensor(T.cc[:], T.cst[:], T.eqs[:, 15:CV:16], A.subtract), ["cst", "eqs"], ["cc"], ("mask", 0))
+        one("v", lambda: V.tensor_tensor(T.acc[:, 0:3 * KS:3], T.lts[:, 15:CS:16], T.eqs[:, CV + 15:C:16], A.add), ["lts", "eqs"],
+            [acc(k, 0)[1] for k in range(KV, KB)], ("mask", 0))
         for k in range(2, KV):
             compare(k)
             if k > GV:
                 add_up(k - GV - 1)
-        for k in range(KV - GV - 1, KV - 1):
+        for k in range(max(0, KV - GV - 1), KV):
             add_up(k)
-        op("v", lambda: V.tensor_tensor_scan(T.cols[:, CV:CV + KV * CS], T.cap1[:], T.mask[:, KV * CV:KV * C], 0.0, A.min, A.add),
-           ["cap1"] + ["mu%d" % k for k in range(KV)], ["cols"])
-        add_up(KV - 1)
-        e = turn(T.colt[:, 0:CS], T.cols[:, CV + KV - 1:CV + KV * CS:KV], ["cols"], ["colt1"])
-        turn(T.colt[:, CS:2 * CS + 32], T.cols[:, KV - 1:KV * (CS + 32):KV], ["cols", "colpad0", "colpad1"], ["colt2"], join=e)
-        op("v", lambda: V.tensor_scalar(T[place][:, 0:KV], T.sums[:, HC - 1:HC * KV:HC], float(HC), None, A.add),
-           ["sum%d" % k for k in range(KV)], [place + "v"])
-        op("v", lambda: V.tensor_tensor_scan(T.colu[:], T.cap2[:], T.colt[:], 0.0, A.min, A.add), ["cap2", "colt1", "colt2"], ["colu"])
-        scatter(0, KV - 2, place + "v")
-        op("v", lambda: V.tensor_tensor(T.acc[:, 0:3 * KS:3], T.colu[:, 0:2 * CS + 32].indirect(T.l_col[:, 0:1]), T.cc[:, KV:KB], A.subtract),
-           ["colu", "l_col", "cc"], ["accc"])
-        scatter(KV - 2, KV, place + "v")
-        op("v", lambda: V.tensor_tensor_scan(T.acce[:], T.turns[:, 1:3 * KS + 1], T.acc[:], 0.0, A.mult, A.add),
-           ["accu%d" % j for j in range(KS)] + ["accl%d" % j for j in range(KS)] + ["accc", "turns"], ["acce"])
-        op("v", lambda: V.tensor_scalar(T[place][:, KV:KB], T.acce[:, 2:3 * KS:3], float(HC), None, A.add), ["acce"], [place + "s"])
+        run_up(0)
+        one("v", lambda: V.tensor_scalar(T[place][:, 0:KV], T.sums[:, HC - 1:HC * KV:HC], float(HC), None, A.add),
+            ["sum%d" % k for k in range(KV)], [place + "v"])
+        for i in range(1, NC):
+            run_up(i)
+        cut = [0, 2, 4, 6, KV]
+        scatter(cut[0], cut[1], place + "v")
+        for i in range(NC):
+            differ(i)
+        scatter(cut[1], cut[2], place + "v")
+        COLS = ["cols%d" % i for i in range(NC)] + ["colpad0", "colpad1"]
+        turn(T.colt[:, 0:CS], T.cols[:, 16:16 + CS], COLS, ["colt1"], (slot, "colt"))
+        turn(T.colt[:, CS:2 * CS + 32], T.cols[:], COLS, ["colt2"], (slot, "colt"))
+        scatter(cut[2], cut[3], place + "v")
+        one("v", lambda: V.tensor_tensor_scan(T.colu[:], T.cap2[:], T.colt[:], 0.0, A.min, A.add), ["cap2", "colt1", "colt2"], ["colu"], "colu")
+        one("v", lambda: V.tensor_tensor_scan(T.acce[:], T.turns[:, 1:97], T.acc[:], 0.0, A.mult, A.add),
+            ["acc%d" % j for j in range(96)] + ["turns"], ["acce"], "colu")
+        scatter(cut[3], cut[4], place + "v")
+        one("v", lambda: V.tensor_tensor(T.pl[:], T.colu[:].indirect(T.l_col[:]), T.acce[:, 2:96:3], A.subtract),
+            ["colu", "l_col0", "l_col1", "acce"], ["pl"])
+        one("v", lambda: V.tensor_scalar(T[place][:, KV:KB], T.pl[:, 0:KS], -1.0, float(HC), A.mult, A.add), ["pl"], [place + "s"])
         scatter(KV, KB, place + "s")
-        e = turn(T.invt[:, 0:448], T.inv[:, o + 16:o + 464], [key], ["invt1"])
-        turn(T.invt[:, 448:928], T.inv[:, o:o + 480], [key], ["invt2"], join=e)
-        op("v", lambda: V.tensor_scalar(T[order][:], T.invt[:, 0:928].indirect(T.l_d[:, 2:4]), float(HC), None, A.add),
-           ["invt1", "invt2", "l_d0", "l_d1"], [order])
+        turn(T.invt[:, 0:C], T.inv[:, o + 16:o + 16 + C], [key], ["invt1"], (slot, "invt"))
+        turn(T.invt[:, C:C + CP], T.inv[:, o:o + CP], [key], ["invt2"], (slot, "invt"))
+        one("v", lambda: V.tensor_scalar(T[order][:], T.invt[:].indirect(T.l_d[:]), 4.0, 4.0 * HC, A.mult, A.add),
+            ["invt1", "invt2", "l_d0", "l_d1"], [order])
 
-    def store_order(slot, buf, out):
-        o = 480 * slot
+    def order_values(slot, buf):
+        o = CP * slot
         op("s", lambda: SC.activation(T[buf][:], T.inv[:, o + 16:o + 16 + C], F.Identity, bias=float(HC)), ["inv%d" % slot], [buf])
-        for k in range(8):
-            op("y", lambda k=k: g.sync.dma_start(out[k:k + 1, :], T[buf][16 * k:16 * k + 1, :]), [buf], out=True)
+
+    def store_order(buf, out, after):
+        op("y", lambda: g.sync.dma_start(out[:], T[buf][0:128:16, :]), [buf] + after, out=True)
 
     plan = engine_plan(T, topo, rank)
     arrive = [sum(2 * len(engine_plan(T, topo, r)[i].get(rank, ())) for r in range(N) if r != rank) for i in range(2)]
 
-    def send(src, dst, i, key):
-        wait("g", writer[key])
+    def send(src, dst, i):
+        name = "%s%d" % (src, i)
+        wait("g", writer[name + "q"])
         for suffix, view in (("_q", u8), ("_s", lambda ap: ap)):
             ts = []
             for d, engines in plan[i].items():
                 rid, pid, _ = topo.addr(T.cores[d])
+                a, z = (S * (d % 2), S * (rank % 2)) if i == 0 else (PIECE[1][2], HC)
                 ts.append(RemoteDMATransfer(dst_ids=[DstId(rid=rid, pnc=pid)], dma_engine_mask=sum(1 << x for x in engines),
-                                            remote_sem=T.sem[("far_", "near_")[i] + dst], src=view(T[src + suffix][:, S * d:S * d + S]),
-                                            dst=view(T[dst + suffix][:, S * rank:S * rank + S])))
+                                            remote_sem=T.sem[("far_", "near_")[i] + dst], src=view(T[name + suffix][:, a:a + S]),
+                                            dst=view(T[dst + suffix][:, z:z + S])))
                 total["sent"] = total.get("sent", 0) + len(engines)
             g.remote_dma_fused(ts, local_sem=T.sem.sent)
 
-    def keep(src, dst):
-        pick(dst, S * rank, S * rank + S, src, C, T.l_own[:, 0:7], [src + "q0", src + "q1", "l_own"], dst)
+    def products(w, home, land, i, blocks, reads):
+        k, n, off, width = PIECE[i]
+        first = 4 if i == 0 else 0
+        if i < 2:
+            PE.wait_ge(T.sem[("far_", "near_")[i] + land], arrive[i])
+        x, a, z, skip = [(land, 0, HC, 0), (land, 3 * S - 128, 3 * S, 128 - S), (home + "2", 0, 128, off)][i]
+        for j, b in enumerate(blocks):
+            mm(first + b, w, 128 * b, x, a, z, reads + ([home + "2q"] if i == 2 else []), (w, i, j // 2 if i == 0 else 0))
+        return first, skip, 16 * k + off, width
 
-    def products(w, x, h, blocks, reads):
-        a = HC * h
-        PE.wait_ge(T.sem[("far_" if h == early else "near_") + x], arrive[0 if h == early else 1])
-        first = 4 if h == early else 0
-        for b in blocks:
-            mm(first + b, w, 128 * b, x, a, a + HC, reads + ([x + "q", x + "s"] if h == late else []))
-        return a, first
-
-    quant("u", T.ut, 0, 128, ["ut"], ["uq"])
-    pick("ur", 0, 128, "u", 128, T.l_u[:, 0:8], ["uq", "l_u"], "ur")
-    op("v", lambda: V.tensor_scalar(T.after[:], T.cidx[:], T.cxt[:, 64:65], None, A.is_gt), ["cidx", "cxt"], ["after"])
+    quant("u", T.ut, 0, 128, ["ut"], ["uq"], "uq")
+    pick("ur", "u")
+    pack_half("x", 0, ["xt0"])
+    lists()
+    pack_half("x", 1, ["xt1"])
     for h in range(2):
-        quant("x", T.xt, HC * h, HC * h + HC, ["xt%d" % h], ["xq%d" % h])
-        scores("ur", "x", h, h == 1, ["urq", "urs", "xq%d" % h])
+        scores("ur", "x", h, h == 1, 0)
     rank_columns("place1", "order1", 0)
-    for b in (0, 1, 2, 3):
-        move("s", plane(T.xp, b), elem(T.xt, b), XT, ["xp%d" % b])
 
-    for i, h in enumerate((early, late)):
-        for q, b in (("v", 0), ("s", 1), ("v", 2), ("s", 3)):
-            gather(q, T.ft, T.xp, b, "order1", HB * h, HB * h + HB, ["xp%d" % b, "order1"], "ft%d%d" % (h, b))
-        quant("f", T.ft, HC * h, HC * h + HC, ["ft%d%d" % (h, b) for b in range(4)], ["fq%d" % h])
-        send("f", "a", i, "fq%d" % h)
+    XS = [(T.xt[:, 64:64 + WIN], XT)] + [(T["x%d" % b][:, 0:WIN], ["x%d" % b]) for b in (1, 2, 3)]
+
+    def sort_x(q, b, i):
+        k, n = PIECE[i][0:2]
+        move(q, elem(T["ft%d" % i], b, 0, 16 * n), XS[b][0].indirect(T.order1[:, k:k + n]), XS[b][1] + ["order1"], ["ft%d%d" % (i, b)],
+             "ft%d" % i, "vs")
+
+    def pack(name, i):
+        quant("%s%d" % (name, i), T["%st%d" % (name, i)], 0, 16 * PIECE[i][1], ["%st%d%d" % (name, i, b) for b in range(4)], ["%s%dq" % (name, i)])
+
+    for q, b in (("v", 0), ("s", 1), ("v", 2), ("s", 3)):
+        sort_x(q, b, 0)
+    sort_x("v", 0, 1)
+    pack("f", 0)
+    send("f", "a", 0)
+    for b in (1, 2, 3):
+        sort_x("s", b, 1)
+    sort_x("v", 0, 2)
+    sort_x("v", 2, 2)
+    pack("f", 1)
+    send("f", "a", 1)
+    sort_x("s", 1, 2)
+    sort_x("s", 3, 2)
     quant("v", T.vt, 0, 128, ["vt"], ["vq"])
-    keep("f", "a")
-    pick("vr", 0, 128, "v", 128, T.l_u[:, 0:8], ["vq", "l_u"], "vr")
-    op("v", lambda: V.memset(T.half[:], 0.5), [], ["half"])
-    quant("e", T.et, 0, 512, ["et%d" % b for b in range(4)], ["eq_"])
-    store_order(0, "oaf", T.oa)
+    pack("f", 2)
+    pick("vr", "v")
 
-    for h in (early, late):
-        a, first = products("w", "a", h, range(4), ["wq", "ws"])
+    def layer(i, on):
+        first, skip, a, n = products("w", "f", "a", i, range(4), ["wq", "ws"])
         for b in range(4):
-            out, src, keys = elem(T.ht, b, a, a + HC), bank(first + b), (["ps%d" % (first + b)], ["ht%d%d" % (h, b)])
-            if b % 2:
+            out, src = elem(T.ht, b, 16 + a, 16 + a + n), bank(first + b, skip, skip + n)
+            keys = (["ps%d" % (first + b)], ["ht%d%d" % (i, b)], "ht%d" % i, "vs")
+            if on[b] == "v":
                 op("v", lambda: V.tensor_scalar(out, src, 0.00390625, None, A.mult), *keys)
             else:
                 op("s", lambda: SC.activation(out, src, F.Identity, scale=0.00390625), *keys)
-        quant("h", T.ht, a, a + HC, ["ht%d%d" % (h, b) for b in range(4)], ["hq%d" % h])
-    for h in (early, late):
-        scores("vr", "h", h, h == late, ["vrq", "vrs", "hq%d" % h])
+
+    HT = ["ht%d%d" % (i, b) for i in range(3) for b in range(4)]
+    layer(2, "svsv")
+    order_values(0, "oaf")
+    quant("e", T.et, 0, 512, ["et%d" % b for b in range(4)], ["eq_"], "em")
+    quant("m", T.mt, 0, 128, ["mt"], ["mq"], "em")
+    layer(0, "svsv")
+    pack_half("h", early, HT[:4])
+    layer(1, "svss")
+    pack_half("h", late, HT[4:])
+    scores("vr", "h", early, False, 1)
+    scores("vr", "h", late, True, 1)
+    for b in (1, 3, 2):
+        op("y", lambda: g.sync.dma_start(T["h%d" % b][:, 0:WIN], T.ht[:, 64 + b:64 + b + WIN]), HT + ["htpad1"], ["h%d" % b], "hcopy", load=True)
+    store_order("oaf", T.oa, [])
     rank_columns("place2", "order2", 1)
-    for b in (0, 1, 3, 2):
-        move("s", plane(T.hp, b), elem(T.ht, b), ["ht0%d" % b, "ht1%d" % b], ["hp%d" % b])
+
+    HS = [(T.ht[:, 64:64 + WIN], HT)] + [(T["h%d" % b][:, 0:WIN], ["h%d" % b]) for b in (1, 2, 3)]
+    P1, P2 = ["place1v", "place1s"], ["place2v", "place2s"]
 
     def sort_h(q, b):
-        move(q, plane(T.hs, b), plane(T.hp, b).indirect(T.order2[:, 0:KB]), ["hp%d" % b, "order2"], ["hs%d" % b])
+        move(q, plane(T.hs, b), HS[b][0].indirect(T.order2[:, 0:KB]), HS[b][1] + ["order2"], ["hs%d" % b])
 
     def scan(b):
         op("v", lambda: V.tensor_tensor_scan(plane(T.rs, b), T.half[:], plane(T.hs, b), 0.0, A.mult, A.max), ["half", "hs%d" % b], ["rs%d" % b])
 
-    def back(q, b, h, a=0, z=HB):
-        key = "tt%d%d%d" % (h, b, a)
-        gather(q, T.tt, T.rs, b, "place2", HB * h + a, HB * h + z, ["rs%d" % b, "place2v", "place2s"], key)
-        return key
+    def back(q, b, i):
+        k, n = PIECE[i][0:2]
+        move(q, elem(T["tt%d" % i], b, 0, 16 * n), plane(T.rs, b).indirect(T.place2[:, k:k + n]), ["rs%d" % b] + P2, ["tt%d%d" % (i, b)],
+             "tt%d" % i, "vs")
 
-    sort_h("v", 0)
-    sort_h("s", 1)
-    sort_h("s", 3)
-    scan(0)
-    scan(1)
-    keys = [back("s", 0, early), back("s", 1, early)]
-    sort_h("v", 2)
-    scan(3)
-    scan(2)
-    keys += [back("s", 3, early), back("v", 2, early)]
-    quant("t", T.tt, HC * early, HC * early + HC, keys, ["tq%d" % early])
-    send("t", "b", 0, "tq%d" % early)
-    keys = [back("s", 0, late), back("s", 1, late), back("v", 2, late), back("s", 3, late, 0, 8), back("v", 3, late, 8, HB)]
-    quant("t", T.tt, HC * late, HC * late + HC, keys, ["tq%d" % late])
-    send("t", "b", 1, "tq%d" % late)
-    keep("t", "b")
-    quant("m", T.mt, 0, 128, ["mt"], ["mq"])
-    store_order(1, "obf", T.ob)
+    for q, b in (("v", 0), ("s", 1), ("s", 3), ("v", 2)):
+        sort_h(q, b)
+    for b in range(4):
+        scan(b)
+    for q, b in (("s", 0), ("s", 1), ("v", 2), ("s", 3)):
+        back(q, b, 0)
+    back("v", 2, 1)
+    pack("t", 0)
+    send("t", "b", 0)
+    for b in (0, 1, 3):
+        back("s", b, 1)
+    back("v", 2, 2)
+    back("v", 3, 2)
+    pack("t", 1)
+    send("t", "b", 1)
+    back("s", 0, 2)
+    back("s", 1, 2)
+    pack("t", 2)
 
-    for h in (early, late):
-        a, first = products("e", "b", h, (0, 2, 1, 3), ["eq_"])
+    for i in (2, 0, 1):
+        first, skip, a, n = products("e", "t", "b", i, (0, 2, 1, 3), ["eq_"])
+        off = PIECE[i][2]
         for b in (0, 1):
-            op("v", lambda: V.tensor_tensor(plane(T.zs, b, a, a + HC), bank(first + b), elem(T.ft, b, a, a + HC), A.add),
-               ["ps%d" % (first + b), "ft%d%d" % (h, b)], ["zs%d%d" % (h, b)])
+            op("v", lambda: V.tensor_tensor(plane(T.zs, b, a, a + n), bank(first + b, skip, skip + n), elem(T["ft%d" % i], b, off, off + n), A.add),
+               ["ps%d" % (first + b), "ft%d%d" % (i, b)], ["zs%d%d" % (i, b)], "zs%d" % i, "vs")
         for b in (2, 3):
-            move("s", plane(T.zs, b, a, a + HC), bank(first + b), ["ps%d" % (first + b)], ["zs%d%d" % (h, b)])
+            move("s", plane(T.zs, b, a, a + n), bank(first + b, skip, skip + n), ["ps%d" % (first + b)], ["zs%d%d" % (i, b)], "zs%d" % i, "vs")
+        if i == 2:
+            order_values(1, "obf")
+    store_order("obf", T.ob, ["zs10"])
 
     def store_y(i):
         a, z = 16 * ZP[i], 16 * ZP[i + 1]
@@ -408,23 +522,31 @@ def rank_program(g, core, T, topo):
         move(q, T.yf[:, a:z], bank(4 + i, 0, z - a), ["ps%d" % (4 + i)], ["y%d" % i])
         op(dq, lambda: Q[dq].dma_start(T.y[:, a:z], T.yf[:, a:z]), ["y%d" % i], out=True)
 
-    for i in range(len(ZP) - 1):
+    def home(q, b, i):
         a, z = ZP[i], ZP[i + 1]
-        for b in range(4):
-            reads = ["zs0%d" % b, "zs1%d" % b, "place1v", "place1s"]
-            if b < 2:
-                gather("s", T.zt, T.zs, b, "place1", a, z, reads, "zt%d%d" % (i, b))
-            else:
-                op("v", lambda: V.tensor_tensor(elem(T.zt, b, 16 * a, 16 * z), plane(T.zs, b).indirect(T.place1[:, a:z]),
-                                                elem(T.xt, b, 16 * a, 16 * z), A.add), reads, ["zt%d%d" % (i, b)])
-        quant("z", T.zt, 16 * a, 16 * z, ["zt%d%d" % (i, b) for b in range(4)], ["zq%d" % i])
-        mm(4 + i, "m", 0, "z", 16 * a, 16 * z, ["mq", "zq%d" % i])
-        op("y", lambda: g.sync.dma_start(T.oc[:, 64 * a:64 * z], u8(T.z_q[:, 16 * a:16 * z])), ["zq%d" % i], out=True)
+        reads, keys = ["zs%d%d" % (j, b) for j in range(3)] + P1, (["zt%d%d" % (i, b)], "zt%d" % i, "vs")
+        out, src = elem(T.zt, b, 16 * a, 16 * z), plane(T.zs, b).indirect(T.place1[:, a:z])
+        if q == "s":
+            move("s", out, src, reads, *keys)
+        else:
+            op("v", lambda: V.tensor_tensor(out, src, elem(T.xt, b, 16 + 16 * a, 16 + 16 * z), A.add), reads, *keys)
+
+    last = len(ZP) - 2
+    for i in range(last + 1):
+        for q, b in (("s", 0), ("s", 1), ("v", 2), ("v", 3)):
+            if i == 0 or b != 2:
+                home(q, b, i)
+        if i < last:
+            home("v", 2, i + 1)
+        a, z = 16 * ZP[i], 16 * ZP[i + 1]
+        quant("z", T.zt, a, z, ["zt%d%d" % (i, b) for b in range(4)], ["zq%d" % i])
+        mm(4 + i, "m", 0, "z", a, z, ["mq", "zq%d" % i])
+        op("y", lambda: g.sync.dma_start(T.oc[:, 4 * a:4 * z], u8(T.z_q[:, a:z])), ["zq%d" % i], out=True)
         if i:
             store_y(i - 1)
     for k in range(4):
-        op("s", lambda: SC.dma_start(T.osc[4 * k:4 * k + 4, :], T.z_s[32 * k:32 * k + 4, :]), ["zq%d" % i for i in range(len(ZP) - 1)], out=True)
-    store_y(len(ZP) - 2)
+        op("s", lambda: SC.dma_start(T.osc[4 * k:4 * k + 4, :], T.z_s[32 * k:32 * k + 4, :]), ["zq%d" % i for i in range(last + 1)], out=True)
+    store_y(last)
 
     g.wait_ge(T.sem.sent, total["sent"])
     for s in sorted(last_on, key=lambda x: last_on[x]):

@@ -4,7 +4,8 @@ from concourse.mybir import dt, AluOpType as A, ActivationFunctionType as F
 C, S, N = 448, 112, 4
 KB = C // 16
 KV = 8
-K0 = 18
+K0 = 20
+AHEAD = [18, 19]
 HM = K0 // 2
 KS, K1, K2 = KB - KV, K0 - KV, KB - K0
 CV, CS, C0, C2 = 16 * KV, 16 * KS, 16 * K0, 16 * K2
@@ -37,7 +38,8 @@ SCRATCH = {
     "ht": ("sbuf", [128, 4 * CP], BF), "hs": ("sbuf", [128, 4 * C], BF), "rs": ("sbuf", [128, 4 * C], BF),
     "zs": ("sbuf", [128, 4 * C], BF), "zt": ("sbuf", [128, 4 * C], BF),
     "ones": ("sbuf", [128, 512], BF), "et": ("sbuf", [128, 2048], BF),
-    "sp": ("sbuf", [128, C], F32), "turn": ("sbuf", [128, C + CP], F32), "dpos": ("sbuf", [128, 32], F32), "dneg": ("sbuf", [128, 32], F32),
+    "sp": ("sbuf", [128, C], F32), "turn": ("sbuf", [128, C + CP], F32),
+    "dpos": ("sbuf", [128, 32], F32), "dneg": ("sbuf", [128, 32], F32), "dfirst": ("sbuf", [128, 32], F32),
     "eq": ("sbuf", [128, C], BF), "eqs": ("sbuf", [128, C], BF), "after": ("sbuf", [128, C], BF), "cidx": ("sbuf", [128, C], BF),
     "lt": ("sbuf", [128, CS], BF), "lts": ("sbuf", [128, CS], BF), "cap1": ("sbuf", [128, CS], BF),
     "vals": ("sbuf", [128, C], BF), "half": ("sbuf", [128, C], BF),
@@ -47,17 +49,17 @@ SCRATCH = {
     "cum": ("sbuf", [128, NC * CW], F16), "cols": ("sbuf", [128, CS + 32], BF),
     "colt": ("sbuf", [128, 2 * CS + 32], BF), "colu": ("sbuf", [128, 2 * CS + 32], BF), "cap2": ("sbuf", [128, 2 * CS + 32], BF),
     "acc": ("sbuf", [128, 96], F32), "acce": ("sbuf", [128, 96], F32), "turns": ("sbuf", [128, 99], F32), "pl": ("sbuf", [128, 32], F32),
-    "inv": ("sbuf", [128, 2 * CP], BF), "invt": ("sbuf", [128, C + CP], BF),
+    "inv": ("sbuf", [128, 2 * CP], BF), "invt": ("sbuf", [128, 2 * CP], BF),
     "oaf": ("sbuf", [128, C], F32), "obf": ("sbuf", [128, C], F32), "yf": ("sbuf", [128, C], F32),
-    "i16": ("sbuf", [128, 8], "int32"), "cx": ("sbuf", [128, 128], F32), "cxt": ("sbuf", [128, 128], F32),
+    "i16": ("sbuf", [128, 8], "int32"), "cx": ("sbuf", [128, 160], F32), "cxt": ("sbuf", [128, 160], F32),
     "l_u": ("sbuf", [128, 8], "uint16"), "l_d": ("sbuf", [128, 2], "uint16"), "l_rep": ("sbuf", [128, 32], "uint16"),
-    "l_col": ("sbuf", [128, 2], "uint16"), "l_p": ("sbuf", [128, 2], "uint16"),
+    "l_col": ("sbuf", [128, 2], "uint16"), "l_p": ("sbuf", [128, 2], "uint16"), "l_i": ("sbuf", [128, 2], "uint16"),
     "place1": ("sbuf", [128, KB], "uint16"), "place2": ("sbuf", [128, KB], "uint16"),
     "order1": ("sbuf", [128, 32], "uint16"), "order2": ("sbuf", [128, 32], "uint16"),
     "ps": ("psum", [128, 4096], F32),
 }
-for _n, _w in (("x", CP), ("u", 128), ("ur", 128), ("v", 128), ("vr", 128), ("m", 128), ("w", 512), ("e", 512),
-               ("f0", HC), ("f1", 128), ("f2", 128), ("a", 3 * S), ("h", CP), ("t0", HC), ("t1", 128), ("t2", 128), ("b", 3 * S), ("z", C)):
+for _n, _w in (("x", CP), ("u", 128), ("ur", 128), ("v", 128), ("vr", 128), ("m", 128), ("w", 512), ("e", 512), ("f0", HC), ("f1", 128), ("f2", 128),
+               ("a", 3 * S + 16), ("h", CP), ("t0", HC), ("t1", 128), ("t2", 128), ("b", 3 * S), ("z", C)):
     SCRATCH[_n + "_q"] = ("sbuf", [128, _w], X4)
     SCRATCH[_n + "_s"] = ("sbuf", [128, _w], U8)
 
@@ -81,10 +83,18 @@ def rank_program(g, core, T, topo):
         return
     Q = {"g": g, "v": g.vector, "s": g.scalar, "t": g.tensor, "y": g.sync}
     V, SC, PE = g.vector, g.scalar, g.tensor
-    late = rank // 2
-    early = 1 - late
-    mate = 2 * late + 1 - rank % 2
-    PIECE = [(HB * early, HB, 0, HC), (HB * late + 6 * (mate % 2), 8, 16 * (mate % 2), S), (HB * late + 6 * (rank % 2), 8, 16 * (rank % 2), S)]
+    mine = rank // 2
+    mate = 2 * mine + 1 - rank % 2
+    PIECE = [(HB * (1 - mine), HB, 0, HC), (HB * mine + 6 * (mate % 2), 8, 16 * (mate % 2), S), (HB * mine + 6 * (rank % 2), 8, 16 * (rank % 2), S)]
+    down = mine == 0
+    BV, BS = (KS, 0) if down else (0, KV)
+    B1, B2 = (K2, 0) if down else (KV, K0)
+
+    def block(role):
+        return KB - 1 - role if down else role
+
+    def span(a, z):
+        return (C - 16 * z, C - 16 * a) if down else (16 * a, 16 * z)
 
     known = {q: set() for q in Q}
     events = []
@@ -182,10 +192,11 @@ def rank_program(g, core, T, topo):
     def plane(t, b, a=0, z=C):
         return t[:, C * b + a:C * b + z]
 
-    op("s", lambda: SC.dma_start(T.ut[:], T.u[:]), [], ["ut"], load=True)
-    op("y", lambda: g.sync.dma_start(T.xt[:, 64:64 + 2 * C], T.x[:, 0:2 * C]), [], ["xt0"], load=True)
-    op("y", lambda: g.sync.dma_start(T.xt[:, 64 + 2 * C:64 + 4 * C], T.x[:, 2 * C:4 * C]), [], ["xt1"], load=True)
     XT = ["xt0", "xt1"]
+    op("s", lambda: SC.dma_start(T.ut[:], T.u[:]), [], ["ut"], load=True)
+    for i in range(2):
+        a = 2 * C * (mine if i == 0 else 1 - mine)
+        op("y", lambda: g.sync.dma_start(T.xt[:, 64 + a:64 + a + 2 * C], T.x[:, a:a + 2 * C]), [], [XT[i]], load=True)
     op("y", lambda: g.sync.dma_start(T.vt[:], T.v[:]), XT, ["vt"], "more", load=True)
     for b in (1, 2, 3):
         op("y", lambda: g.sync.dma_start(T["x%d" % b][:, 0:WIN], T.x[:, b:b + WIN]), [], ["x%d" % b], "more", load=True)
@@ -196,135 +207,165 @@ def rank_program(g, core, T, topo):
     def iota(out, pattern, base, keys, tag):
         op("g", lambda: g.iota(out, pattern, base, 0, allow_small_or_imprecise_dtypes=True), [], keys, tag)
 
-    def zero(out, n, keys, tag):
-        iota(out, [[0, n]], 0, keys, tag)
+    def zero(t, a, z, keys, tag):
+        iota(t[:, a:z], [[0, z - a]], 0, keys, tag)
 
-    for a, far, base in ((0, C + 16, 0), (64, CS + 16, 15)):
+    op("g", lambda: g.iota(T.i16[:], [[16, 8]], 0, 0), [], ["i16"])
+    for a, far, base in ((0, C + 16, 0), (64, CS + 16, 15), (128, HC + 16, 0)):
         iota(T.cx[:, a:a + 16], [[32, 8], [16 + far, 2]], base, ["cx%da" % a], "cx")
         iota(T.cx[:, a + 16:a + 32], [[32, 8], [16 - far, 2]], base + far, ["cx%db" % a], "cx")
     iota(T.cx[:, 32:64], [[0, 2], [1, 16]], 0, ["cx32"], "cx")
     iota(T.cx[:, 96:128], [[1, 32]], 0, ["cx96"], "cx")
-    op("g", lambda: g.iota(T.i16[:], [[16, 8]], 0, 0), [], ["i16"])
+    zero(T.acc, 0, 96, ["acc%d" % k for k in range(96)], None)
     iota(T.cidx[:], [[0, KB], [1, 16]], 0, ["cidx"], None)
-    zero(T.lt[:, C0 - CV:CS], C2, ["ltpad"], "g1")
-    iota(T.cap1[:], [[-16, KS], [1, 16]], HC + LOW - 15 - CV, ["cap1"], "g1")
-    iota(T.cst[:], [[0, KV]], -HC - 1, ["cst"], "g1")
-    zero(T.ma[:, HM * CV:HM * 16 * HM], HM * (16 * HM - CV), ["mu%d" % k for k in range(HM)], "g1")
-    zero(T.acc[:], 96, ["acc%d" % k for k in range(96)], "g1")
-    zero(T.mb[:, 0:HM * (C0 - CV)], HM * (C0 - CV), ["mu%d" % k for k in range(HM, K0)], None)
+    zero(T.lt, 16 * (B2 - BS), 16 * (B2 - BS) + C2, ["ltpad"], "g1")
+    iota(T.cap1[:], [[-16, KS], [1, 16]], HC - 15 - 16 * BS + (-LOW if down else LOW), ["cap1"], "g1")
+    iota(T.cst[:], [[0, KV]], -HC if down else -HC - 1, ["cst"], "g1")
     iota(T.vals[:], [[1, C]], -HC, ["vals"], "g2")
     iota(T.turns[:], [[0, 33], [1, 3]], -1, ["turns"], "g2")
     iota(T.cap2[:], [[0, 2 * KS + 2], [32, 16]], -LOW, ["cap2"], "g2")
-    zero(T.cols[:, 0:16], 16, ["colpad0"], "g2")
-    zero(T.cols[:, CS + 16:CS + 32], 16, ["colpad1"], "g2")
-    zero(T.inv[:], 2 * CP, ["inv0", "inv1"], "g2")
+    zero(T.cols, 0, 16, ["colpad0"], "g2")
+    zero(T.cols, CS + 16, CS + 32, ["colpad1"], "g2")
+    for i, (a, z) in enumerate(((0, 16), (CP - 16, CP + 16), (2 * CP - 16, 2 * CP))):
+        zero(T.inv, a, z, ["invpad%d" % i], "g2")
     iota(T.ones[:], [[0, 512]], 1, ["ones"], None)
     for b in range(4):
         op("g", lambda b=b: g.affine_select(T.et[:, 512 * b:512 * b + 512], T.ones[:], [[1, 512]], A.is_equal, 0.0, -b, -4),
            ["ones"], ["et%d" % b], "et")
 
+    def fill(ap, value, keys, tag="v0"):
+        op("v", lambda: V.memset(ap, value), [], keys, tag)
+
+    def listed(out, a, more, top, key, tag):
+        op("v", lambda: V.tensor_scalar(out, T.cxt[:, a:a + 1], float(more), float(top), A.add, A.min), ["cxt"], [key], tag)
+
     for t in ("xt", "ht"):
-        op("v", lambda: V.memset(T[t][:, 0:64], 0.0), [], [t + "pad0"], "v0")
-        op("v", lambda: V.memset(T[t][:, 4 * CP - 64:4 * CP], 0.0), [], [t + "pad1"], "v0")
-    op("v", lambda: V.memset(T.half[:], 0.5), [], ["half"], "v0")
-    op("v", lambda: V.memset(T.cum[:, HM - 1:NC * CW:CW], 0.0), [], ["cumpad"], "v0")
-    turn(T.cxt[:], T.cx[:], ["cx0a", "cx0b", "cx32", "cx64a", "cx64b", "cx96"], ["cxt"])
+        fill(T[t][:, 0:64], 0.0, [t + "pad0"])
+        fill(T[t][:, 4 * CP - 64:4 * CP], 0.0, [t + "pad1"])
+    fill(T.cum[:, HM - 1:NC * CW:CW], 0.0, ["cumpad"])
+    a, z = span(KV, K0)
+    fill(T.mb[:, HM * (a - 16 * BS):HM * (z - 16 * BS)], 0.0, ["mzb"])
     op("v", lambda: V.tensor_copy(T.l_u[:], T.i16[:]), ["i16"], ["l_u"], "uq")
-    op("v", lambda: V.tensor_copy(T.l_p[:, 0:1], T.cxt[:, 96:97]), ["cxt"], ["l_p"], "uq")
-    for name, a, top in (("l_d", 0, C + CP - 1), ("l_col", 64, 2 * CS + 31)):
-        op("v", lambda: V.tensor_copy(T[name][:, 0:1], T.cxt[:, a:a + 1]), ["cxt"], [name + "0"], "v1")
-        op("v", lambda: V.tensor_scalar(T[name][:, 1:2], T.cxt[:, a:a + 1], 256.0, float(top), A.add, A.min), ["cxt"], [name + "1"], "v1")
+    quant("u", T.ut, 0, 128, ["ut"], ["uq"], "uq")
+    a, z = span(KV, HM)
+    fill(T.ma[:, HM * a:HM * z], 0.0, ["mza"], "v2")
+    turn(T.cxt[:], T.cx[:], ["cx0a", "cx0b", "cx32", "cx64a", "cx64b", "cx96", "cx128a", "cx128b"], ["cxt"])
 
-    def lists():
-        src = T.cx[:, 0:32].indirect(T.l_p[:, 0:1])
-        op("v", lambda: V.tensor_copy(T.l_rep[:, 0:16], src), ["l_p"], ["l_rep0"], "v1")
-        op("v", lambda: V.tensor_scalar(T.l_rep[:, 16:32], src, 256.0, C + CP - 1.0, A.add, A.min), ["l_p"], ["l_rep1"], "v1")
-        op("v", lambda: V.tensor_scalar(T.after[:], T.cidx[:], T.cxt[:, 32:33], None, A.is_gt), ["cidx", "cxt"], ["after"], "v1")
+    def pack_half(name, i, reads):
+        a = CP // 2 * (mine if i == 0 else 1 - mine)
+        quant(name, T[name + "t"], a, a + CP // 2, reads + [name + "tpad0", name + "tpad1"], ["%sq%d" % (name, i)])
 
-    def pack_half(name, h, reads):
-        a = CP // 2 * h
-        quant(name, T[name + "t"], a, a + CP // 2, reads + [name + "tpad%d" % h], [name + "q%d" % h])
+    def scores(w, x, i, first):
+        h = mine if i == 0 else 1 - mine
+        lo = h * (HC if i else HC + 16)
+        hi = CP if h else HC + (32 if i else 16)
+        s0, s1 = (lo, hi) if i else (lo + 16 * h, hi - 16 * (1 - h))
+        p = 16 + HC * h - lo
+        reads = [w + "q", w + "s"] + ["%sq%d" % (x, j) for j in range(i + 1)]
+        mm(first, w, 0, x, lo, hi, reads)
+        mm(first + 1, w, 0, x, lo, hi, reads)
+        turn(T.turn[:, HC * h:HC * h + HC], bank(first, p, p + HC), ["ps%d" % first], ["turna%d" % i], ("turn", x, i))
+        turn(T.turn[:, C + s0:C + s1], bank(first, s0 - lo, s1 - lo), ["ps%d" % first], ["turnb%d" % i], ("turn", x, i))
+        move("s", T.sp[:, HC * h:HC * h + HC], bank(first + 1, p, p + HC), ["ps%d" % (first + 1)], ["sp%d" % i])
 
-    def scores(w, x, h, last, slot):
-        a, i = HC * h, 6 if last else 4
-        lo = h * (HC if last else HC + 16)
-        hi = CP if h else HC + (32 if last else 16)
-        s0, s1 = (lo if last else lo + 16 * h), (hi if last or h else hi - 16)
-        tn, sp, reads = "turn%d" % slot, "sp%d" % slot, [w + "q", w + "s", x + "q%d" % h]
-        mm(i, w, 0, x, lo, hi, reads + ([x + "q%d" % (1 - h)] if last else []))
-        mm(i + 1, w, 0, x, a + 16, a + 16 + HC, reads)
-        move("s", T.sp[:, a:a + HC], bank(i + 1), ["ps%d" % (i + 1)], ["sp%d" % h], sp)
-        turn(T.turn[:, a:a + HC], bank(i, a + 16 - lo, a + 16 - lo + HC), ["ps%d" % i], ["turna%d" % h], tn)
-        turn(T.turn[:, C + s0:C + s1], bank(i, s0 - lo, s1 - lo), ["ps%d" % i], ["turnb%d" % h], tn)
-
-    def rank_columns(place, order, slot):
-        turned = ["turna0", "turna1", "turnb0", "turnb1", "l_d0", "l_d1", "l_rep0", "l_rep1"]
+    def sorter(slot):
+        place, order = "place%d" % (slot + 1), "order%d" % (slot + 1)
+        TURNED = ["turna0", "turnb0", "turna1", "turnb1", "l_d0", "l_d1", "l_rep0", "l_rep1"]
         SP = ["sp0", "sp1"]
+        ahead = AHEAD if slot else []
+        n = 12 if slot else 0
+        EQ = ((0, n), (n, KB)) if down else ((KB - n, KB), (0, KB - n))
 
         def one(q, make, reads, writes, tag=None):
             op(q, make, reads, writes, None if tag is None else (slot, tag))
 
-        def row(k, a, z):
-            if k < HM:
-                return T.ma[:, HM * a + k:HM * z:HM]
-            return T.mb[:, HM * (a - CV) + k - HM:HM * (z - CV):HM]
+        def row(role, a, z):
+            if role < HM:
+                return T.ma[:, HM * a + role:HM * z:HM]
+            return T.mb[:, HM * (a - 16 * BS) + role - HM:HM * (z - 16 * BS):HM]
 
-        def acc(k, j):
-            i = 3 * (k - KV) + j
+        def acc(role, j):
+            i = 3 * (block(role) - BS) + j
             return T.acc[:, i:i + 1], "acc%d" % i
 
-        one("s", lambda: SC.activation(T.dneg[:], T.turn[:].indirect(T.l_d[:]), F.Identity, scale=-1.0), turned, ["dneg"])
-        move("v", T.dpos[:], T.turn[:].indirect(T.l_d[:]), turned, ["dpos"])
-
-        def sign(k):
-            if k < K0:
-                out, a = T.sgn[:, SG[k - KV]:SG[k - KV + 1]], 16 * k + 16
+        def sign(role, pivots, reads, tag):
+            k = block(role)
+            if role < K0:
+                out, (a, z) = T.sgn[:, SG[role - KV]:SG[role - KV + 1]], span(role + 1, KB)
             else:
-                out, a = T.sg2[:, C2 * (k - K0):C2 * (k - K0 + 1)], C0
-            one("s", lambda: SC.activation(out, T.sp[:, a:C], F.Sign, bias=T.dneg[:, k:k + 1]),
-                SP + ["dneg"], ["sgl%d" % k, "sgu%d" % k], ("sign", (k - KV) // GS))
+                out, (a, z) = T.sg2[:, C2 * (role - K0):C2 * (role - K0 + 1)], span(K0, KB)
+            one("s", lambda: SC.activation(out, T.sp[:, a:z], F.Sign, bias=T[pivots][:, k:k + 1]),
+                reads + [pivots], ["sgl%d" % role, "sgu%d" % role], ("sign", tag))
 
-        def count(k):
-            (lo_sum, lo_key), (up_sum, up_key) = acc(k, 1), acc(k, 2)
-            if k < K0:
-                one("s", lambda: SC.activation(row(k, 16 * k + 16, C), T.sgn[:, SG[k - KV]:SG[k - KV + 1]], F.Relu, accum_out=up_sum),
-                    ["sgu%d" % k], ["mu%d" % k, up_key], ("up", k < max(HM, CUTS[1] - 1)))
+        def count(role):
+            (lo_sum, lo_key), (up_sum, up_key) = acc(role, 1), acc(role, 2)
+            if role < K0:
+                a, z = span(role + 1, KB)
+                sums, key = (lo_sum, lo_key) if down else (up_sum, up_key)
+                one("s", lambda: SC.activation(row(role, a, z), T.sgn[:, SG[role - KV]:SG[role - KV + 1]], F.Relu, scale=-1.0 if down else 1.0,
+                                               accum_out=sums), ["sgu%d" % role, "mza" if role < HM else "mzb"], ["mu%d" % role, key],
+                    ("up", role < CUTS[1] - 1 or role in ahead))
                 return
-            a, n = C2 * (k - K0), 16 * (k - K0) + 16
+            a, n = C2 * (role - K0), 16 * (block(role) - B2) + 16
             lo, up = T.sg2[:, a:a + n], T.sg2[:, a + n:a + C2]
-            one("s", lambda: SC.activation(lo, lo, F.Relu, scale=-1.0, accum_out=lo_sum), [], ["sgl%d" % k, lo_key], "count")
+            one("s", lambda: SC.activation(lo, lo, F.Relu, scale=-1.0, accum_out=lo_sum), [], ["sgl%d" % role, lo_key], "count")
             if n < C2:
-                one("s", lambda: SC.activation(up, up, F.Relu, accum_out=up_sum), [], ["sgu%d" % k, up_key], "count")
+                one("s", lambda: SC.activation(up, up, F.Relu, accum_out=up_sum), [], ["sgu%d" % role, up_key], "count")
 
-        starts = list(range(KV, KB, GS))
-        for i in range(len(starts) + 1):
-            for k in range(KV + GS * i, min(KB, KV + GS * i + GS)):
-                sign(k)
-            if i:
-                for k in range(starts[i - 1], min(KB, starts[i - 1] + GS)):
-                    count(k)
+        def pivots(name):
+            one("s", lambda: SC.activation(T[name][:], T.turn[:].indirect(T.l_d[:]), F.Identity, scale=-1.0), TURNED, [name])
 
-        def compare(k):
+        def equal(i):
+            a, z = EQ[i]
+            one("v", lambda: V.tensor_tensor(T.eq[:, 16 * a:16 * z], T.turn[:].indirect(T.l_rep[:, a:z]), T.sp[:, 16 * a:16 * z], A.is_equal),
+                SP[:i + 1] + TURNED, ["eq%d" % i], ("eq", i))
+
+        def first_signs():
+            pivots("dfirst")
+            for role in ahead:
+                sign(role, "dfirst", SP[:1], "first")
+
+        def first_equal():
+            equal(0)
+            count(ahead[0])
+
+        def on_scalar():
+            for role in ahead[1:]:
+                count(role)
+            for part, (a, z) in enumerate(((KV, K0), (K0, KB))):
+                roles = [k for k in range(a, z) if k not in ahead]
+                groups = [roles[i:i + GS] for i in range(0, len(roles), GS)]
+                for i in range(len(groups) + 1):
+                    for role in groups[i] if i < len(groups) else []:
+                        sign(role, "dneg", SP, (part, i))
+                    for role in groups[i - 1] if i else []:
+                        count(role)
+
+        def compare(role):
+            k = block(role)
             n = 16 * k + 16
-            for a, z, how, name in ((0, n, A.is_ge, "ml%d"), (n, C, A.is_gt, "mu%d")):
-                one("v", lambda: V.tensor_scalar(row(k, a, z), T.sp[:, a:z], T.dpos[:, k:k + 1], None, how),
-                    SP + ["dpos"], [name % k], ("mask", k // GV))
+            for a, z, how, name in ((0, n, A.is_lt if down else A.is_ge, "ml%d"), (n, C, A.is_le if down else A.is_gt, "mu%d")):
+                if a < z:
+                    one("v", lambda: V.tensor_scalar(row(role, a, z), T.sp[:, a:z], T.dpos[:, k:k + 1], None, how),
+                        SP + ["dpos"], [name % role], ("mask", role // GV))
 
-        def add_up(k):
-            one("v", lambda: V.tensor_tensor_scan(T.sums[:, HC * k:HC * k + HC], row(k, 0, HC), row(k, HC, C), T.cc[:, k:k + 1], A.add, A.add),
-                ["ml%d" % k, "mu%d" % k, "cc"], ["sum%d" % k], "sum")
+        def add_up(role):
+            j = block(role) - BV
+            one("v", lambda: V.tensor_tensor_scan(T.sums[:, HC * j:HC * j + HC], row(role, 0, HC), row(role, HC, C), T.cc[:, j:j + 1], A.add, A.add),
+                ["ml%d" % role, "mu%d" % role, "cc"], ["sum%d" % role], "sum")
 
         def run_up(i):
-            a, z = 16 * CUTS[i], 16 * CUTS[i + 1]
+            a, z = span(CUTS[i], CUTS[i + 1])
             o = CW * i + HM
-            one("v", lambda: V.tensor_tensor_scan(T.cum[:, o:o + HM * (z - a)], T.ma[:, HM * a:HM * z], T.mb[:, HM * (a - CV):HM * (z - CV)],
-                                                  0.0, A.add, A.add), ["mu%d" % k for k in range(K0) if k < max(HM, CUTS[i + 1] - 1)], ["cum%d" % i], "cum")
+            one("v", lambda: V.tensor_tensor_scan(T.cum[:, o:o + HM * (z - a)], T.ma[:, HM * a:HM * z], T.mb[:, HM * (a - 16 * BS):HM * (z - 16 * BS)],
+                                                  0.0, A.add, A.add),
+                ["m%s%d" % (s, k) for s in "lu" for k in range(K0) if k < CUTS[i + 1] - 1] + ["mza", "mzb"], ["cum%d" % i], "cum")
 
         def differ(i):
-            a, z = 16 * CUTS[i], 16 * CUTS[i + 1]
+            a, z = span(CUTS[i], CUTS[i + 1])
             o = CW * i + HM - 1
             n = HM * (z - a)
-            one("v", lambda: V.tensor_tensor_scan(T.cols[:, 16 + a - CV:16 + z - CV], T.cum[:, o + HM:o + n + 1:HM], T.cum[:, o:o + n:HM],
+            one("v", lambda: V.tensor_tensor_scan(T.cols[:, 16 + a - 16 * BS:16 + z - 16 * BS], T.cum[:, o + HM:o + n + 1:HM], T.cum[:, o:o + n:HM],
                                                   0.0, A.max, A.subtract), ["cum%d" % i, "cumpad"], ["cols%d" % i], "cols")
 
         o = CP * slot
@@ -333,47 +374,60 @@ def rank_program(g, core, T, topo):
         def scatter(a, z, part):
             one("v", lambda: V.tensor_copy(T.inv[:, o + 16:o + 16 + C].indirect(T[place][:, a:z]), T.vals[:, 16 * a:16 * z]), [part, "vals"], [key])
 
-        one("v", lambda: V.tensor_tensor(T.eq[:], T.turn[:].indirect(T.l_rep[:, 0:KB]), T.sp[:], A.is_equal), SP + turned, ["eq"], "eq")
-        one("v", lambda: V.tensor_tensor(T.lt[:, 0:C0 - CV], T.turn[:].indirect(T.l_rep[:, KV:K0]), T.sp[:, CV:C0], A.is_gt), SP + turned, ["lt"], "eq")
-        compare(0)
-        one("v", lambda: V.tensor_tensor_scan(T.eqs[:], T.eq[:], T.after[:], 0.0, A.add, A.mult), ["eq", "after"], ["eqs"], "eqs")
-        one("v", lambda: V.tensor_tensor_scan(T.lts[:], T.cap1[:], T.lt[:], 0.0 + HC + LOW, A.min, A.add), ["lt", "ltpad", "cap1"], ["lts"], "eqs")
-        compare(1)
-        one("v", lambda: V.tensor_tensor(T.cc[:], T.cst[:], T.eqs[:, 15:CV:16], A.subtract), ["cst", "eqs"], ["cc"], ("mask", 0))
-        one("v", lambda: V.tensor_tensor(T.acc[:, 0:3 * KS:3], T.lts[:, 15:CS:16], T.eqs[:, CV + 15:C:16], A.add), ["lts", "eqs"],
-            [acc(k, 0)[1] for k in range(KV, KB)], ("mask", 0))
-        for k in range(2, KV):
-            compare(k)
-            if k > GV:
-                add_up(k - GV - 1)
-        for k in range(max(0, KV - GV - 1), KV):
-            add_up(k)
-        run_up(0)
-        one("v", lambda: V.tensor_scalar(T[place][:, 0:KV], T.sums[:, HC - 1:HC * KV:HC], float(HC), None, A.add),
-            ["sum%d" % k for k in range(KV)], [place + "v"])
-        for i in range(1, NC):
-            run_up(i)
-        cut = [0, 2, 4, 6, KV]
-        scatter(cut[0], cut[1], place + "v")
-        for i in range(NC):
-            differ(i)
-        scatter(cut[1], cut[2], place + "v")
-        COLS = ["cols%d" % i for i in range(NC)] + ["colpad0", "colpad1"]
-        turn(T.colt[:, 0:CS], T.cols[:, 16:16 + CS], COLS, ["colt1"], (slot, "colt"))
-        turn(T.colt[:, CS:2 * CS + 32], T.cols[:], COLS, ["colt2"], (slot, "colt"))
-        scatter(cut[2], cut[3], place + "v")
-        one("v", lambda: V.tensor_tensor_scan(T.colu[:], T.cap2[:], T.colt[:], 0.0, A.min, A.add), ["cap2", "colt1", "colt2"], ["colu"], "colu")
-        one("v", lambda: V.tensor_tensor_scan(T.acce[:], T.turns[:, 1:97], T.acc[:], 0.0, A.mult, A.add),
-            ["acc%d" % j for j in range(96)] + ["turns"], ["acce"], "colu")
-        scatter(cut[3], cut[4], place + "v")
-        one("v", lambda: V.tensor_tensor(T.pl[:], T.colu[:].indirect(T.l_col[:]), T.acce[:, 2:96:3], A.subtract),
-            ["colu", "l_col0", "l_col1", "acce"], ["pl"])
-        one("v", lambda: V.tensor_scalar(T[place][:, KV:KB], T.pl[:, 0:KS], -1.0, float(HC), A.mult, A.add), ["pl"], [place + "s"])
-        scatter(KV, KB, place + "s")
-        turn(T.invt[:, 0:C], T.inv[:, o + 16:o + 16 + C], [key], ["invt1"], (slot, "invt"))
-        turn(T.invt[:, C:C + CP], T.inv[:, o:o + CP], [key], ["invt2"], (slot, "invt"))
-        one("v", lambda: V.tensor_scalar(T[order][:], T.invt[:].indirect(T.l_d[:]), 4.0, 4.0 * HC, A.mult, A.add),
-            ["invt1", "invt2", "l_d0", "l_d1"], [order])
+        def rest():
+            pivots("dneg")
+            move("v", T.dpos[:], T.turn[:].indirect(T.l_d[:]), TURNED, ["dpos"])
+            on_scalar()
+            equal(1)
+            one("v", lambda: V.tensor_tensor(T.lt[:, 16 * (B1 - BS):16 * (B1 - BS + K1)], T.turn[:].indirect(T.l_rep[:, B1:B1 + K1]),
+                                             T.sp[:, 16 * B1:16 * (B1 + K1)], A.is_gt), SP + TURNED, ["lt"], ("eq", 1))
+            compare(0)
+            one("v", lambda: V.tensor_tensor_scan(T.eqs[:], T.eq[:], T.after[:], 0.0, A.add, A.mult), ["eq0", "eq1", "after"], ["eqs"], "eqs")
+            one("v", lambda: V.tensor_tensor_scan(T.lts[:], T.cap1[:], T.lt[:], 0.0 + HC + LOW, A.min, A.add), ["lt", "ltpad", "cap1"], ["lts"], "eqs")
+            compare(1)
+            one("v", lambda: V.tensor_tensor(T.cc[:], T.cst[:], T.eqs[:, 16 * BV + 15:16 * (BV + KV):16], A.add if down else A.subtract),
+                ["cst", "eqs"], ["cc"], ("mask", 0))
+            one("v", lambda: V.tensor_tensor(T.acc[:, 0:3 * KS:3], T.lts[:, 15:CS:16], T.eqs[:, 16 * BS + 15:16 * (BS + KS):16], A.add), ["lts", "eqs"],
+                ["acc%d" % (3 * k) for k in range(KS)], ("mask", 0))
+            for k in range(2, KV):
+                compare(k)
+            for k in range(KV - 3):
+                add_up(k)
+            for i in range(NC):
+                run_up(i)
+            for k in range(KV - 3, KV):
+                add_up(k)
+            for i in range(NC):
+                differ(i)
+            one("v", lambda: V.tensor_scalar(T[place][:, BV:BV + KV], T.sums[:, HC - 1:HC * KV:HC], -1.0 if down else 1.0,
+                                             HC - 1.0 if down else float(HC), A.mult, A.add), ["sum%d" % k for k in range(KV)], [place + "v"])
+            if slot == 0:
+                listed(T.l_col[:, 0:1], 64, 0, 2 * CS + 31, "l_col0", "v3")
+                listed(T.l_col[:, 1:2], 64, 256, 2 * CS + 31, "l_col1", "v3")
+                listed(T.l_i[:, 0:1], 128, 0, CP - 1, "l_i", "v3")
+            COLS = ["cols%d" % i for i in range(NC)] + ["colpad0", "colpad1"]
+            turn(T.colt[:, 0:CS], T.cols[:, 16:16 + CS], COLS, ["colt1"], (slot, "colt"))
+            turn(T.colt[:, CS:2 * CS + 32], T.cols[:], COLS, ["colt2"], (slot, "colt"))
+            scatter(BV, BV + KV // 2, place + "v")
+            one("v", lambda: V.tensor_tensor_scan(T.colu[:], T.cap2[:], T.colt[:], 0.0, A.min, A.add), ["cap2", "colt1", "colt2"], ["colu"], "colu")
+            one("v", lambda: V.tensor_tensor_scan(T.acce[:], T.turns[:, 1:97], T.acc[:], 0.0, A.mult, A.add),
+                ["acc%d" % j for j in range(96)] + ["turns"], ["acce"], "colu")
+            one("v", lambda: V.tensor_tensor(T.pl[:], T.colu[:].indirect(T.l_col[:]), T.acce[:, 2:96:3], A.add if down else A.subtract),
+                ["colu", "l_col0", "l_col1", "acce"], ["pl"])
+            scatter(BV + KV // 2, BV + KV, place + "v")
+            one("v", lambda: V.tensor_scalar(T[place][:, BS:BS + KS], T.pl[:, 0:KS], 1.0 if down else -1.0, float(HC), A.mult, A.add), ["pl"], [place + "s"])
+            scatter(BS, BS + KS, place + "s")
+            pads = [key, "invpad0", "invpad1", "invpad2"]
+            halves = (0, 1) if slot else (mine, 1 - mine)
+            for h in halves:
+                a = o + HC * h
+                turn(T.invt[:, CP * h:CP * h + HC], T.inv[:, a + 16:a + 16 + HC], pads, ["invt1%d" % h], (slot, "invt", h))
+                turn(T.invt[:, CP * h + HC:CP * h + CP], T.inv[:, a:a + HC + 32], pads, ["invt2%d" % h], (slot, "invt", h))
+            for h in halves:
+                one("v", lambda: V.tensor_scalar(T[order][:, 16 * h:16 * h + 16], T.invt[:, CP * h:CP * h + CP].indirect(T.l_i[:, 0:1]), 4.0, 4.0 * HC,
+                                                 A.mult, A.add), ["invt1%d" % h, "invt2%d" % h, "l_i"], [order + str(h)])
+
+        return first_signs, first_equal, rest
 
     def order_values(slot, buf):
         o = CP * slot
@@ -401,108 +455,122 @@ def rank_program(g, core, T, topo):
 
     def products(w, home, land, i, blocks, reads):
         k, n, off, width = PIECE[i]
-        first = 4 if i == 0 else 0
+        first = 4 if i == 0 or (i == 2 and land == "a") else 0
         if i < 2:
             PE.wait_ge(T.sem[("far_", "near_")[i] + land], arrive[i])
-        x, a, z, skip = [(land, 0, HC, 0), (land, 3 * S - 128, 3 * S, 128 - S), (home + "2", 0, 128, off)][i]
+        near = (land, HC, HC + 128, 0, ["apadq", "apads"]) if land == "a" else (land, 3 * S - 128, 3 * S, 128 - S, [])
+        x, a, z, skip, more = [(land, 0, HC, 0, []), near, (home + "2", 0, 128, off, [home + "2q"])][i]
         for j, b in enumerate(blocks):
-            mm(first + b, w, 128 * b, x, a, z, reads + ([home + "2q"] if i == 2 else []), (w, i, j // 2 if i == 0 else 0))
+            mm(first + b, w, 128 * b, x, a, z, reads + more, (w, i, j // 2))
         return first, skip, 16 * k + off, width
 
-    quant("u", T.ut, 0, 128, ["ut"], ["uq"], "uq")
     pick("ur", "u")
-    pack_half("x", 0, ["xt0"])
-    lists()
-    pack_half("x", 1, ["xt1"])
-    for h in range(2):
-        scores("ur", "x", h, h == 1, 0)
-    rank_columns("place1", "order1", 0)
+    pack_half("x", 0, [XT[0]])
+    op("v", lambda: V.tensor_copy(T.l_p[:, 0:1], T.cxt[:, 96:97]), ["cxt"], ["l_p"])
+    listed(T.l_d[:, 0:1], 0, 0, C + CP - 1, "l_d0", "v1")
+    listed(T.l_d[:, 1:2], 0, 256, C + CP - 1, "l_d1", "v1")
+    pack_half("x", 1, [XT[1]])
+    for j in range(2):
+        op("v", lambda: V.tensor_scalar(T.l_rep[:, 16 * j:16 * j + 16], T.cx[:, 0:32].indirect(T.l_p[:, 0:1]), 256.0 * j, C + CP - 1.0, A.add, A.min),
+           ["l_p"], ["l_rep%d" % j], "v1")
+    scores("ur", "x", 0, 4)
+    scores("ur", "x", 1, 6)
+    op("v", lambda: V.tensor_scalar(T.after[:], T.cidx[:], T.cxt[:, 32:33], None, A.is_gt), ["cidx", "cxt"], ["after"], "v2")
+    pad = 0 if down else CP - 16
+    op("y", lambda: g.sync.dma_start(u8(T.a_q[:, 3 * S:3 * S + 16]), u8(T.x_q[:, pad:pad + 16])), ["xq0"], ["apadq"], "apad", load=True)
+    op("y", lambda: g.sync.dma_start(T.a_s[:, 3 * S:3 * S + 16], T.x_s[:, pad:pad + 16]), ["xq0"], ["apads"], "apad", load=True)
+    sorter(0)[2]()
 
     XS = [(T.xt[:, 64:64 + WIN], XT)] + [(T["x%d" % b][:, 0:WIN], ["x%d" % b]) for b in (1, 2, 3)]
 
     def sort_x(q, b, i):
         k, n = PIECE[i][0:2]
-        move(q, elem(T["ft%d" % i], b, 0, 16 * n), XS[b][0].indirect(T.order1[:, k:k + n]), XS[b][1] + ["order1"], ["ft%d%d" % (i, b)],
+        k += 2 * (k // HB)
+        move(q, elem(T["ft%d" % i], b, 0, 16 * n), XS[b][0].indirect(T.order1[:, k:k + n]), XS[b][1] + ["order1%d" % (k // 16)], ["ft%d%d" % (i, b)],
              "ft%d" % i, "vs")
 
     def pack(name, i):
         quant("%s%d" % (name, i), T["%st%d" % (name, i)], 0, 16 * PIECE[i][1], ["%st%d%d" % (name, i, b) for b in range(4)], ["%s%dq" % (name, i)])
 
-    for q, b in (("v", 0), ("s", 1), ("v", 2), ("s", 3)):
-        sort_x(q, b, 0)
-    sort_x("v", 0, 1)
+    for q, b, i in (("v", 0, 1), ("s", 1, 1), ("v", 2, 1), ("s", 3, 1), ("v", 0, 0)):
+        sort_x(q, b, i)
+    pack("f", 1)
+    send("f", "a", 1)
+    for q, b, i in (("s", 1, 0), ("s", 3, 0), ("v", 2, 0), ("v", 0, 2)):
+        sort_x(q, b, i)
     pack("f", 0)
     send("f", "a", 0)
     for b in (1, 2, 3):
-        sort_x("s", b, 1)
-    sort_x("v", 0, 2)
-    sort_x("v", 2, 2)
-    pack("f", 1)
-    send("f", "a", 1)
-    sort_x("s", 1, 2)
-    sort_x("s", 3, 2)
-    quant("v", T.vt, 0, 128, ["vt"], ["vq"])
+        sort_x("s", b, 2)
     pack("f", 2)
+    quant("v", T.vt, 0, 128, ["vt"], ["vq"])
+    quant("e", T.et, 0, 512, ["et%d" % b for b in range(4)], ["eq_"])
     pick("vr", "v")
+    fill(T.half[:], 0.5, ["half"], None)
 
-    def layer(i, on):
+    HT = ["ht%d%d" % (i, b) for i in range(3) for b in range(4)]
+
+    def layer(i):
         first, skip, a, n = products("w", "f", "a", i, range(4), ["wq", "ws"])
         for b in range(4):
             out, src = elem(T.ht, b, 16 + a, 16 + a + n), bank(first + b, skip, skip + n)
             keys = (["ps%d" % (first + b)], ["ht%d%d" % (i, b)], "ht%d" % i, "vs")
-            if on[b] == "v":
+            if b % 2:
                 op("v", lambda: V.tensor_scalar(out, src, 0.00390625, None, A.mult), *keys)
             else:
                 op("s", lambda: SC.activation(out, src, F.Identity, scale=0.00390625), *keys)
 
-    HT = ["ht%d%d" % (i, b) for i in range(3) for b in range(4)]
-    layer(2, "svsv")
-    order_values(0, "oaf")
-    quant("e", T.et, 0, 512, ["et%d" % b for b in range(4)], ["eq_"], "em")
-    quant("m", T.mt, 0, 128, ["mt"], ["mq"], "em")
-    layer(0, "svsv")
-    pack_half("h", early, HT[:4])
-    layer(1, "svss")
-    pack_half("h", late, HT[4:])
-    scores("vr", "h", early, False, 1)
-    scores("vr", "h", late, True, 1)
+    first_signs, first_equal, rest = sorter(1)
+    layer(2)
+    layer(1)
+    pack_half("h", 0, HT[4:])
+    layer(0)
+    scores("vr", "h", 0, 0)
+    first_signs()
+    pack_half("h", 1, HT[:4])
+    first_equal()
+    scores("vr", "h", 1, 2)
     for b in (1, 3, 2):
         op("y", lambda: g.sync.dma_start(T["h%d" % b][:, 0:WIN], T.ht[:, 64 + b:64 + b + WIN]), HT + ["htpad1"], ["h%d" % b], "hcopy", load=True)
+    rest()
+    order_values(0, "oaf")
     store_order("oaf", T.oa, [])
-    rank_columns("place2", "order2", 1)
 
     HS = [(T.ht[:, 64:64 + WIN], HT)] + [(T["h%d" % b][:, 0:WIN], ["h%d" % b]) for b in (1, 2, 3)]
     P1, P2 = ["place1v", "place1s"], ["place2v", "place2s"]
 
-    def sort_h(q, b):
-        move(q, plane(T.hs, b), HS[b][0].indirect(T.order2[:, 0:KB]), HS[b][1] + ["order2"], ["hs%d" % b])
+    def sort_h(q, b, a, z):
+        k = 2 * (a // HB)
+        move(q, plane(T.hs, b, 16 * a, 16 * z), HS[b][0].indirect(T.order2[:, a + k:z + k]), HS[b][1] + ["order2%d" % (a // HB)], ["hs%d_%d" % (b, a)],
+             "hs%d" % b, "vs")
 
     def scan(b):
-        op("v", lambda: V.tensor_tensor_scan(plane(T.rs, b), T.half[:], plane(T.hs, b), 0.0, A.mult, A.max), ["half", "hs%d" % b], ["rs%d" % b])
+        op("v", lambda: V.tensor_tensor_scan(plane(T.rs, b), T.half[:], plane(T.hs, b), 0.0, A.mult, A.max),
+           ["half"] + ["hs%d_%d" % (b, a) for a in (0, 8, HB)], ["rs%d" % b])
 
     def back(q, b, i):
         k, n = PIECE[i][0:2]
         move(q, elem(T["tt%d" % i], b, 0, 16 * n), plane(T.rs, b).indirect(T.place2[:, k:k + n]), ["rs%d" % b] + P2, ["tt%d%d" % (i, b)],
              "tt%d" % i, "vs")
 
-    for q, b in (("v", 0), ("s", 1), ("s", 3), ("v", 2)):
-        sort_h(q, b)
-    for b in range(4):
+    for q, b, a, z in (("v", 0, 0, HB), ("s", 1, 0, HB), ("v", 0, HB, KB), ("s", 1, HB, KB), ("s", 3, 0, HB), ("s", 3, HB, KB),
+                       ("v", 2, 8, HB), ("v", 2, HB, KB), ("s", 2, 0, 8)):
+        sort_h(q, b, a, z)
+    for b in (0, 1, 3, 2):
         scan(b)
-    for q, b in (("s", 0), ("s", 1), ("v", 2), ("s", 3)):
-        back(q, b, 0)
-    back("v", 2, 1)
+    for q, b, i in (("s", 0, 0), ("s", 1, 0), ("v", 3, 0), ("v", 2, 0), ("v", 2, 1)):
+        back(q, b, i)
     pack("t", 0)
     send("t", "b", 0)
-    for b in (0, 1, 3):
-        back("s", b, 1)
-    back("v", 2, 2)
-    back("v", 3, 2)
+    for q, b, i in (("s", 0, 1), ("s", 1, 1), ("s", 3, 1), ("v", 2, 2)):
+        back(q, b, i)
     pack("t", 1)
     send("t", "b", 1)
-    back("s", 0, 2)
-    back("s", 1, 2)
+    for q, b in (("s", 0), ("s", 1), ("v", 3)):
+        back(q, b, 2)
     pack("t", 2)
+    quant("m", T.mt, 0, 128, ["mt"], ["mq"])
+    order_values(1, "obf")
 
     for i in (2, 0, 1):
         first, skip, a, n = products("e", "t", "b", i, (0, 2, 1, 3), ["eq_"])
@@ -512,8 +580,6 @@ def rank_program(g, core, T, topo):
                ["ps%d" % (first + b), "ft%d%d" % (i, b)], ["zs%d%d" % (i, b)], "zs%d" % i, "vs")
         for b in (2, 3):
             move("s", plane(T.zs, b, a, a + n), bank(first + b, skip, skip + n), ["ps%d" % (first + b)], ["zs%d%d" % (i, b)], "zs%d" % i, "vs")
-        if i == 2:
-            order_values(1, "obf")
     store_order("obf", T.ob, ["zs10"])
 
     def store_y(i):

from concourse.bass import DstId, RemoteDMATransfer
from concourse.mybir import dt, AluOpType as A, ActivationFunctionType as F

C, S, N = 448, 112, 4
KB = C // 16
KV = 8
K0 = 20
AHEAD = [18, 19]
HM = K0 // 2
KS, K1, K2 = KB - KV, K0 - KV, KB - K0
CV, CS, C0, C2 = 16 * KV, 16 * KS, 16 * K0, 16 * K2
HC, HB = C // 2, KB // 2
CP = C + 32
WIN = 4 * C - 3
LOW = 64
ZP = [0, 18, 28]
GS, GV = 4, 4
X4, U8, BF, F32, F16 = "float8_e4m3fn_x4", "uint8", "bfloat16", "float32", "float16"

CUTS = [KV]
_s = 0
for _k in range(KV, KB):
    if _s + 16 * min(_k, K0) > 2048:
        CUTS.append(_k)
        _s = 0
    _s += 16 * min(_k, K0)
CUTS.append(KB)
NC = len(CUTS) - 1
CW = HM * (1 + 16 * max(CUTS[_k + 1] - CUTS[_k] for _k in range(NC)))
SG = [sum(C - 16 * (j + 1) for j in range(KV, k)) for k in range(KV, K0 + 1)]

SCRATCH = {
    "xt": ("sbuf", [128, 4 * CP], BF), "ut": ("sbuf", [128, 512], BF), "vt": ("sbuf", [128, 512], BF), "mt": ("sbuf", [128, 512], BF),
    "x1": ("sbuf", [128, 4 * C], BF), "x2": ("sbuf", [128, 4 * C], BF), "x3": ("sbuf", [128, 4 * C], BF),
    "h1": ("sbuf", [128, 4 * C], BF), "h2": ("sbuf", [128, 4 * C], BF), "h3": ("sbuf", [128, 4 * C], BF),
    "ft0": ("sbuf", [128, 2 * C], BF), "ft1": ("sbuf", [128, 512], BF), "ft2": ("sbuf", [128, 512], BF),
    "tt0": ("sbuf", [128, 2 * C], BF), "tt1": ("sbuf", [128, 512], BF), "tt2": ("sbuf", [128, 512], BF),
    "ht": ("sbuf", [128, 4 * CP], BF), "hs": ("sbuf", [128, 4 * C], BF), "rs": ("sbuf", [128, 4 * C], BF),
    "zs": ("sbuf", [128, 4 * C], BF), "zt": ("sbuf", [128, 4 * C], BF),
    "ones": ("sbuf", [128, 512], BF), "et": ("sbuf", [128, 2048], BF),
    "sp": ("sbuf", [128, C], F32), "turn": ("sbuf", [128, C + CP], F32),
    "dpos": ("sbuf", [128, 32], F32), "dneg": ("sbuf", [128, 32], F32), "dfirst": ("sbuf", [128, 32], F32),
    "eq": ("sbuf", [128, C], BF), "eqs": ("sbuf", [128, C], BF), "after": ("sbuf", [128, C], BF), "cidx": ("sbuf", [128, C], BF),
    "lt": ("sbuf", [128, CS], BF), "lts": ("sbuf", [128, CS], BF), "cap1": ("sbuf", [128, CS], BF),
    "vals": ("sbuf", [128, C], BF), "half": ("sbuf", [128, C], BF),
    "cst": ("sbuf", [128, KV], F32), "cc": ("sbuf", [128, KV], BF),
    "ma": ("sbuf", [128, HM * C], BF), "mb": ("sbuf", [128, HM * CS], BF),
    "sgn": ("sbuf", [128, SG[-1]], BF), "sg2": ("sbuf", [128, K2 * C2], BF), "sums": ("sbuf", [128, KV * HC], BF),
    "cum": ("sbuf", [128, NC * CW], F16), "cols": ("sbuf", [128, CS + 32], BF),
    "colt": ("sbuf", [128, 2 * CS + 32], BF), "colu": ("sbuf", [128, 2 * CS + 32], BF), "cap2": ("sbuf", [128, 2 * CS + 32], BF),
    "acc": ("sbuf", [128, 96], F32), "acce": ("sbuf", [128, 96], F32), "turns": ("sbuf", [128, 99], F32), "pl": ("sbuf", [128, 32], F32),
    "inv": ("sbuf", [128, 2 * CP], BF), "invt": ("sbuf", [128, 2 * CP], BF),
    "oaf": ("sbuf", [128, C], F32), "obf": ("sbuf", [128, C], F32), "yf": ("sbuf", [128, C], F32),
    "i16": ("sbuf", [128, 8], "int32"), "cx": ("sbuf", [128, 160], F32), "cxt": ("sbuf", [128, 160], F32),
    "l_u": ("sbuf", [128, 8], "uint16"), "l_d": ("sbuf", [128, 2], "uint16"), "l_rep": ("sbuf", [128, 32], "uint16"),
    "l_col": ("sbuf", [128, 2], "uint16"), "l_p": ("sbuf", [128, 2], "uint16"), "l_i": ("sbuf", [128, 2], "uint16"),
    "place1": ("sbuf", [128, KB], "uint16"), "place2": ("sbuf", [128, KB], "uint16"),
    "order1": ("sbuf", [128, 32], "uint16"), "order2": ("sbuf", [128, 32], "uint16"),
    "ps": ("psum", [128, 4096], F32),
}
for _n, _w in (("x", CP), ("u", 128), ("ur", 128), ("v", 128), ("vr", 128), ("m", 128), ("w", 512), ("e", 512), ("f0", HC), ("f1", 128), ("f2", 128),
               ("a", 3 * S + 16), ("h", CP), ("t0", HC), ("t1", 128), ("t2", 128), ("b", 3 * S), ("z", C)):
    SCRATCH[_n + "_q"] = ("sbuf", [128, _w], X4)
    SCRATCH[_n + "_s"] = ("sbuf", [128, _w], U8)

POOL = ["e%d" % i for i in range(130)]
LOADS = ["ld%d" % i for i in range(8)]
SEMAPHORES = POOL + LOADS + ["far_a", "near_a", "far_b", "near_b", "sent", "outs"]


def engine_plan(T, topo, r):
    src = T.cores[r]
    far = [d for d in range(N) if d // 2 != r // 2]
    near = [d for d in range(N) if d // 2 == r // 2 and d != r][0]
    eng = [e for e in topo.engines(src, T.cores[near]) if all(e in topo.engines(src, T.cores[d]) for d in far)]
    q = len(eng) // 2
    return [{far[0]: eng[:q], far[1]: eng[q:]}, {near: eng}]


def rank_program(g, core, T, topo):
    rank = T.rank_of(core)
    if rank is None:
        return
    Q = {"g": g, "v": g.vector, "s": g.scalar, "t": g.tensor, "y": g.sync}
    V, SC, PE = g.vector, g.scalar, g.tensor
    mine = rank // 2
    mate = 2 * mine + 1 - rank % 2
    PIECE = [(HB * (1 - mine), HB, 0, HC), (HB * mine + 6 * (mate % 2), 8, 16 * (mate % 2), S), (HB * mine + 6 * (rank % 2), 8, 16 * (rank % 2), S)]
    down = mine == 0
    BV, BS = (KS, 0) if down else (0, KV)
    B1, B2 = (K2, 0) if down else (KV, K0)

    def block(role):
        return KB - 1 - role if down else role

    def span(a, z):
        return (C - 16 * z, C - 16 * a) if down else (16 * a, 16 * z)

    known = {q: set() for q in Q}
    events = []
    total, last_on, waited, tags = {}, {}, {}, {}
    writer, readers = {}, {}
    closed = set()
    loads = list(LOADS)

    def wait(q, e):
        if e is None or e in known[q]:
            return
        s, n, k = events[e][0:3]
        closed.add(e)
        Q[q].wait_ge(T.sem[s], n)
        waited[s] = max(waited.get(s, 0), n)
        known[q].add(e)
        known[q].update(k)

    def op(q, make, reads=(), writes=(), tag=None, on=None, load=False, out=False):
        need = set()
        for k in reads:
            if k in writer:
                need.add(writer[k])
            if k.startswith("ps"):
                need.update(e for e, qq in readers.get(k, []) if qq != q)
        for k in writes:
            if k in writer:
                need.add(writer[k])
            need.update(e for e, qq in readers.get(k, []))
        e = tags.get(tag)
        assert e is None or (e not in need and e not in closed), tag
        for x in sorted(need, reverse=True):
            wait(q, x)
        if out:
            make().then_inc(T.sem.outs, 16)
            total["outs"] = total.get("outs", 0) + 16
            return
        step = 16 if load else 1
        if e is None:
            if load:
                s = loads.pop(0)
            else:
                free = [x for x in POOL if x in last_on and all(last_on[x] in known[y] for y in (on or q))]
                s = min(free, key=lambda x: last_on[x]) if free else [x for x in POOL if x not in last_on][0]
            e = len(events)
            events.append([s, 0, set(), last_on.get(s)])
            last_on[s] = e
            if tag is not None:
                tags[tag] = e
        s = events[e][0]
        assert events[e][3] is None or events[e][3] in known[q], tag
        make().then_inc(T.sem[s], step)
        total[s] = total.get(s, 0) + step
        events[e][1] = total[s]
        events[e][2].update(known[q])
        for k in reads:
            readers.setdefault(k, []).append((e, q))
        for k in writes:
            writer[k] = e
            readers[k] = []

    def bank(i, a=0, b=HC):
        return T.ps[:, 512 * i + a:512 * i + b]

    def u8(ap):
        return ap.bitcast(dt.uint8)

    def u32(ap):
        return ap.bitcast(dt.uint32)

    def quant(name, src, a, b, reads, writes, tag=None):
        op("v", lambda: V.quantize_mx(T[name + "_q"][:, a:b], T[name + "_s"][:, a:b], src[:, 4 * a:4 * b]), reads, writes, tag)

    def mm(i, w, wa, x, a, b, reads, tag=None):
        op("t", lambda: PE.matmul_mx(bank(i, 0, b - a), T[w + "_q"][:, wa:wa + 128], T[w + "_s"][:, wa:wa + 128],
                                     T[x + "_q"][:, a:b], T[x + "_s"][:, a:b], True, True), reads, ["ps%d" % i], tag)

    def pick(dst, src):
        lst, reads = T.l_u[:, 0:8], [src + "q", "l_u"]
        op("v", lambda: V.tensor_copy(u32(T[dst + "_q"][:]), u32(T[src + "_q"][:]).indirect(lst)), reads, [dst + "q"], dst, "vs")
        op("s", lambda: SC.activation(T[dst + "_s"][:], T[src + "_s"][:].indirect(lst), F.Copy), reads, [dst + "s"], dst, "vs")

    def move(q, out, in_, reads, writes, tag=None, on=None):
        if q == "v":
            op("v", lambda: V.tensor_copy(out, in_), reads, writes, tag, on)
        else:
            op("s", lambda: SC.activation(out, in_, F.Copy), reads, writes, tag, on)

    def turn(out, in_, reads, writes, tag=None):
        op("v", lambda: V.transpose(out, in_), reads, writes, tag)

    def elem(t, b, a=0, z=C):
        return t[:, 4 * a + b:4 * z:4]

    def plane(t, b, a=0, z=C):
        return t[:, C * b + a:C * b + z]

    XT = ["xt0", "xt1"]
    op("s", lambda: SC.dma_start(T.ut[:], T.u[:]), [], ["ut"], load=True)
    for i in range(2):
        a = 2 * C * (mine if i == 0 else 1 - mine)
        op("y", lambda: g.sync.dma_start(T.xt[:, 64 + a:64 + a + 2 * C], T.x[:, a:a + 2 * C]), [], [XT[i]], load=True)
    op("y", lambda: g.sync.dma_start(T.vt[:], T.v[:]), XT, ["vt"], "more", load=True)
    for b in (1, 2, 3):
        op("y", lambda: g.sync.dma_start(T["x%d" % b][:, 0:WIN], T.x[:, b:b + WIN]), [], ["x%d" % b], "more", load=True)
    op("y", lambda: g.sync.dma_start(u8(T.w_q[:]), T.wc[:]), [], ["wq"], "more", load=True)
    op("y", lambda: g.sync.dma_start(T.w_s[:], T.ws[:]), [], ["ws"], "more", load=True)
    op("y", lambda: g.sync.dma_start(T.mt[:], T.m[:]), [], ["mt"], "more", load=True)

    def iota(out, pattern, base, keys, tag):
        op("g", lambda: g.iota(out, pattern, base, 0, allow_small_or_imprecise_dtypes=True), [], keys, tag)

    def zero(t, a, z, keys, tag):
        iota(t[:, a:z], [[0, z - a]], 0, keys, tag)

    op("g", lambda: g.iota(T.i16[:], [[16, 8]], 0, 0), [], ["i16"])
    for a, far, base in ((0, C + 16, 0), (64, CS + 16, 15), (128, HC + 16, 0)):
        iota(T.cx[:, a:a + 16], [[32, 8], [16 + far, 2]], base, ["cx%da" % a], "cx")
        iota(T.cx[:, a + 16:a + 32], [[32, 8], [16 - far, 2]], base + far, ["cx%db" % a], "cx")
    iota(T.cx[:, 32:64], [[0, 2], [1, 16]], 0, ["cx32"], "cx")
    iota(T.cx[:, 96:128], [[1, 32]], 0, ["cx96"], "cx")
    zero(T.acc, 0, 96, ["acc%d" % k for k in range(96)], None)
    iota(T.cidx[:], [[0, KB], [1, 16]], 0, ["cidx"], None)
    zero(T.lt, 16 * (B2 - BS), 16 * (B2 - BS) + C2, ["ltpad"], "g1")
    iota(T.cap1[:], [[-16, KS], [1, 16]], HC - 15 - 16 * BS + (-LOW if down else LOW), ["cap1"], "g1")
    iota(T.cst[:], [[0, KV]], -HC if down else -HC - 1, ["cst"], "g1")
    iota(T.vals[:], [[1, C]], -HC, ["vals"], "g2")
    iota(T.turns[:], [[0, 33], [1, 3]], -1, ["turns"], "g2")
    iota(T.cap2[:], [[0, 2 * KS + 2], [32, 16]], -LOW, ["cap2"], "g2")
    zero(T.cols, 0, 16, ["colpad0"], "g2")
    zero(T.cols, CS + 16, CS + 32, ["colpad1"], "g2")
    for i, (a, z) in enumerate(((0, 16), (CP - 16, CP + 16), (2 * CP - 16, 2 * CP))):
        zero(T.inv, a, z, ["invpad%d" % i], "g2")
    iota(T.ones[:], [[0, 512]], 1, ["ones"], None)
    for b in range(4):
        op("g", lambda b=b: g.affine_select(T.et[:, 512 * b:512 * b + 512], T.ones[:], [[1, 512]], A.is_equal, 0.0, -b, -4),
           ["ones"], ["et%d" % b], "et")

    def fill(ap, value, keys, tag="v0"):
        op("v", lambda: V.memset(ap, value), [], keys, tag)

    def listed(out, a, more, top, key, tag):
        op("v", lambda: V.tensor_scalar(out, T.cxt[:, a:a + 1], float(more), float(top), A.add, A.min), ["cxt"], [key], tag)

    for t in ("xt", "ht"):
        fill(T[t][:, 0:64], 0.0, [t + "pad0"])
        fill(T[t][:, 4 * CP - 64:4 * CP], 0.0, [t + "pad1"])
    fill(T.cum[:, HM - 1:NC * CW:CW], 0.0, ["cumpad"])
    a, z = span(KV, K0)
    fill(T.mb[:, HM * (a - 16 * BS):HM * (z - 16 * BS)], 0.0, ["mzb"])
    op("v", lambda: V.tensor_copy(T.l_u[:], T.i16[:]), ["i16"], ["l_u"], "uq")
    quant("u", T.ut, 0, 128, ["ut"], ["uq"], "uq")
    a, z = span(KV, HM)
    fill(T.ma[:, HM * a:HM * z], 0.0, ["mza"], "v2")
    turn(T.cxt[:], T.cx[:], ["cx0a", "cx0b", "cx32", "cx64a", "cx64b", "cx96", "cx128a", "cx128b"], ["cxt"])

    def pack_half(name, i, reads):
        a = CP // 2 * (mine if i == 0 else 1 - mine)
        quant(name, T[name + "t"], a, a + CP // 2, reads + [name + "tpad0", name + "tpad1"], ["%sq%d" % (name, i)])

    def scores(w, x, i, first):
        h = mine if i == 0 else 1 - mine
        lo = h * (HC if i else HC + 16)
        hi = CP if h else HC + (32 if i else 16)
        s0, s1 = (lo, hi) if i else (lo + 16 * h, hi - 16 * (1 - h))
        p = 16 + HC * h - lo
        reads = [w + "q", w + "s"] + ["%sq%d" % (x, j) for j in range(i + 1)]
        mm(first, w, 0, x, lo, hi, reads)
        mm(first + 1, w, 0, x, lo, hi, reads)
        turn(T.turn[:, HC * h:HC * h + HC], bank(first, p, p + HC), ["ps%d" % first], ["turna%d" % i], ("turn", x, i))
        turn(T.turn[:, C + s0:C + s1], bank(first, s0 - lo, s1 - lo), ["ps%d" % first], ["turnb%d" % i], ("turn", x, i))
        move("s", T.sp[:, HC * h:HC * h + HC], bank(first + 1, p, p + HC), ["ps%d" % (first + 1)], ["sp%d" % i])

    def sorter(slot):
        place, order = "place%d" % (slot + 1), "order%d" % (slot + 1)
        TURNED = ["turna0", "turnb0", "turna1", "turnb1", "l_d0", "l_d1", "l_rep0", "l_rep1"]
        SP = ["sp0", "sp1"]
        ahead = AHEAD if slot else []
        n = 12 if slot else 0
        EQ = ((0, n), (n, KB)) if down else ((KB - n, KB), (0, KB - n))

        def one(q, make, reads, writes, tag=None):
            op(q, make, reads, writes, None if tag is None else (slot, tag))

        def row(role, a, z):
            if role < HM:
                return T.ma[:, HM * a + role:HM * z:HM]
            return T.mb[:, HM * (a - 16 * BS) + role - HM:HM * (z - 16 * BS):HM]

        def acc(role, j):
            i = 3 * (block(role) - BS) + j
            return T.acc[:, i:i + 1], "acc%d" % i

        def sign(role, pivots, reads, tag):
            k = block(role)
            if role < K0:
                out, (a, z) = T.sgn[:, SG[role - KV]:SG[role - KV + 1]], span(role + 1, KB)
            else:
                out, (a, z) = T.sg2[:, C2 * (role - K0):C2 * (role - K0 + 1)], span(K0, KB)
            one("s", lambda: SC.activation(out, T.sp[:, a:z], F.Sign, bias=T[pivots][:, k:k + 1]),
                reads + [pivots], ["sgl%d" % role, "sgu%d" % role], ("sign", tag))

        def count(role):
            (lo_sum, lo_key), (up_sum, up_key) = acc(role, 1), acc(role, 2)
            if role < K0:
                a, z = span(role + 1, KB)
                sums, key = (lo_sum, lo_key) if down else (up_sum, up_key)
                one("s", lambda: SC.activation(row(role, a, z), T.sgn[:, SG[role - KV]:SG[role - KV + 1]], F.Relu, scale=-1.0 if down else 1.0,
                                               accum_out=sums), ["sgu%d" % role, "mza" if role < HM else "mzb"], ["mu%d" % role, key],
                    ("up", role < CUTS[1] - 1 or role in ahead))
                return
            a, n = C2 * (role - K0), 16 * (block(role) - B2) + 16
            lo, up = T.sg2[:, a:a + n], T.sg2[:, a + n:a + C2]
            one("s", lambda: SC.activation(lo, lo, F.Relu, scale=-1.0, accum_out=lo_sum), [], ["sgl%d" % role, lo_key], "count")
            if n < C2:
                one("s", lambda: SC.activation(up, up, F.Relu, accum_out=up_sum), [], ["sgu%d" % role, up_key], "count")

        def pivots(name):
            one("s", lambda: SC.activation(T[name][:], T.turn[:].indirect(T.l_d[:]), F.Identity, scale=-1.0), TURNED, [name])

        def equal(i):
            a, z = EQ[i]
            one("v", lambda: V.tensor_tensor(T.eq[:, 16 * a:16 * z], T.turn[:].indirect(T.l_rep[:, a:z]), T.sp[:, 16 * a:16 * z], A.is_equal),
                SP[:i + 1] + TURNED, ["eq%d" % i], ("eq", i))

        def first_signs():
            pivots("dfirst")
            for role in ahead:
                sign(role, "dfirst", SP[:1], "first")

        def first_equal():
            equal(0)
            count(ahead[0])

        def on_scalar():
            for role in ahead[1:]:
                count(role)
            for part, (a, z) in enumerate(((KV, K0), (K0, KB))):
                roles = [k for k in range(a, z) if k not in ahead]
                groups = [roles[i:i + GS] for i in range(0, len(roles), GS)]
                for i in range(len(groups) + 1):
                    for role in groups[i] if i < len(groups) else []:
                        sign(role, "dneg", SP, (part, i))
                    for role in groups[i - 1] if i else []:
                        count(role)

        def compare(role):
            k = block(role)
            n = 16 * k + 16
            for a, z, how, name in ((0, n, A.is_lt if down else A.is_ge, "ml%d"), (n, C, A.is_le if down else A.is_gt, "mu%d")):
                if a < z:
                    one("v", lambda: V.tensor_scalar(row(role, a, z), T.sp[:, a:z], T.dpos[:, k:k + 1], None, how),
                        SP + ["dpos"], [name % role], ("mask", role // GV))

        def add_up(role):
            j = block(role) - BV
            one("v", lambda: V.tensor_tensor_scan(T.sums[:, HC * j:HC * j + HC], row(role, 0, HC), row(role, HC, C), T.cc[:, j:j + 1], A.add, A.add),
                ["ml%d" % role, "mu%d" % role, "cc"], ["sum%d" % role], "sum")

        def run_up(i):
            a, z = span(CUTS[i], CUTS[i + 1])
            o = CW * i + HM
            one("v", lambda: V.tensor_tensor_scan(T.cum[:, o:o + HM * (z - a)], T.ma[:, HM * a:HM * z], T.mb[:, HM * (a - 16 * BS):HM * (z - 16 * BS)],
                                                  0.0, A.add, A.add),
                ["m%s%d" % (s, k) for s in "lu" for k in range(K0) if k < CUTS[i + 1] - 1] + ["mza", "mzb"], ["cum%d" % i], "cum")

        def differ(i):
            a, z = span(CUTS[i], CUTS[i + 1])
            o = CW * i + HM - 1
            n = HM * (z - a)
            one("v", lambda: V.tensor_tensor_scan(T.cols[:, 16 + a - 16 * BS:16 + z - 16 * BS], T.cum[:, o + HM:o + n + 1:HM], T.cum[:, o:o + n:HM],
                                                  0.0, A.max, A.subtract), ["cum%d" % i, "cumpad"], ["cols%d" % i], "cols")

        o = CP * slot
        key = "inv%d" % slot

        def scatter(a, z, part):
            one("v", lambda: V.tensor_copy(T.inv[:, o + 16:o + 16 + C].indirect(T[place][:, a:z]), T.vals[:, 16 * a:16 * z]), [part, "vals"], [key])

        def rest():
            pivots("dneg")
            move("v", T.dpos[:], T.turn[:].indirect(T.l_d[:]), TURNED, ["dpos"])
            on_scalar()
            equal(1)
            one("v", lambda: V.tensor_tensor(T.lt[:, 16 * (B1 - BS):16 * (B1 - BS + K1)], T.turn[:].indirect(T.l_rep[:, B1:B1 + K1]),
                                             T.sp[:, 16 * B1:16 * (B1 + K1)], A.is_gt), SP + TURNED, ["lt"], ("eq", 1))
            compare(0)
            one("v", lambda: V.tensor_tensor_scan(T.eqs[:], T.eq[:], T.after[:], 0.0, A.add, A.mult), ["eq0", "eq1", "after"], ["eqs"], "eqs")
            one("v", lambda: V.tensor_tensor_scan(T.lts[:], T.cap1[:], T.lt[:], 0.0 + HC + LOW, A.min, A.add), ["lt", "ltpad", "cap1"], ["lts"], "eqs")
            compare(1)
            one("v", lambda: V.tensor_tensor(T.cc[:], T.cst[:], T.eqs[:, 16 * BV + 15:16 * (BV + KV):16], A.add if down else A.subtract),
                ["cst", "eqs"], ["cc"], ("mask", 0))
            one("v", lambda: V.tensor_tensor(T.acc[:, 0:3 * KS:3], T.lts[:, 15:CS:16], T.eqs[:, 16 * BS + 15:16 * (BS + KS):16], A.add), ["lts", "eqs"],
                ["acc%d" % (3 * k) for k in range(KS)], ("mask", 0))
            for k in range(2, KV):
                compare(k)
            for k in range(KV - 3):
                add_up(k)
            for i in range(NC):
                run_up(i)
            for k in range(KV - 3, KV):
                add_up(k)
            for i in range(NC):
                differ(i)
            one("v", lambda: V.tensor_scalar(T[place][:, BV:BV + KV], T.sums[:, HC - 1:HC * KV:HC], -1.0 if down else 1.0,
                                             HC - 1.0 if down else float(HC), A.mult, A.add), ["sum%d" % k for k in range(KV)], [place + "v"])
            if slot == 0:
                listed(T.l_col[:, 0:1], 64, 0, 2 * CS + 31, "l_col0", "v3")
                listed(T.l_col[:, 1:2], 64, 256, 2 * CS + 31, "l_col1", "v3")
                listed(T.l_i[:, 0:1], 128, 0, CP - 1, "l_i", "v3")
            COLS = ["cols%d" % i for i in range(NC)] + ["colpad0", "colpad1"]
            turn(T.colt[:, 0:CS], T.cols[:, 16:16 + CS], COLS, ["colt1"], (slot, "colt"))
            turn(T.colt[:, CS:2 * CS + 32], T.cols[:], COLS, ["colt2"], (slot, "colt"))
            scatter(BV, BV + KV // 2, place + "v")
            one("v", lambda: V.tensor_tensor_scan(T.colu[:], T.cap2[:], T.colt[:], 0.0, A.min, A.add), ["cap2", "colt1", "colt2"], ["colu"], "colu")
            one("v", lambda: V.tensor_tensor_scan(T.acce[:], T.turns[:, 1:97], T.acc[:], 0.0, A.mult, A.add),
                ["acc%d" % j for j in range(96)] + ["turns"], ["acce"], "colu")
            one("v", lambda: V.tensor_tensor(T.pl[:], T.colu[:].indirect(T.l_col[:]), T.acce[:, 2:96:3], A.add if down else A.subtract),
                ["colu", "l_col0", "l_col1", "acce"], ["pl"])
            scatter(BV + KV // 2, BV + KV, place + "v")
            one("v", lambda: V.tensor_scalar(T[place][:, BS:BS + KS], T.pl[:, 0:KS], 1.0 if down else -1.0, float(HC), A.mult, A.add), ["pl"], [place + "s"])
            scatter(BS, BS + KS, place + "s")
            pads = [key, "invpad0", "invpad1", "invpad2"]
            halves = (0, 1) if slot else (mine, 1 - mine)
            for h in halves:
                a = o + HC * h
                turn(T.invt[:, CP * h:CP * h + HC], T.inv[:, a + 16:a + 16 + HC], pads, ["invt1%d" % h], (slot, "invt", h))
                turn(T.invt[:, CP * h + HC:CP * h + CP], T.inv[:, a:a + HC + 32], pads, ["invt2%d" % h], (slot, "invt", h))
            for h in halves:
                one("v", lambda: V.tensor_scalar(T[order][:, 16 * h:16 * h + 16], T.invt[:, CP * h:CP * h + CP].indirect(T.l_i[:, 0:1]), 4.0, 4.0 * HC,
                                                 A.mult, A.add), ["invt1%d" % h, "invt2%d" % h, "l_i"], [order + str(h)])

        return first_signs, first_equal, rest

    def order_values(slot, buf):
        o = CP * slot
        op("s", lambda: SC.activation(T[buf][:], T.inv[:, o + 16:o + 16 + C], F.Identity, bias=float(HC)), ["inv%d" % slot], [buf])

    def store_order(buf, out, after):
        op("y", lambda: g.sync.dma_start(out[:], T[buf][0:128:16, :]), [buf] + after, out=True)

    plan = engine_plan(T, topo, rank)
    arrive = [sum(2 * len(engine_plan(T, topo, r)[i].get(rank, ())) for r in range(N) if r != rank) for i in range(2)]

    def send(src, dst, i):
        name = "%s%d" % (src, i)
        wait("g", writer[name + "q"])
        for suffix, view in (("_q", u8), ("_s", lambda ap: ap)):
            ts = []
            for d, engines in plan[i].items():
                rid, pid, _ = topo.addr(T.cores[d])
                a, z = (S * (d % 2), S * (rank % 2)) if i == 0 else (PIECE[1][2], HC)
                ts.append(RemoteDMATransfer(dst_ids=[DstId(rid=rid, pnc=pid)], dma_engine_mask=sum(1 << x for x in engines),
                                            remote_sem=T.sem[("far_", "near_")[i] + dst], src=view(T[name + suffix][:, a:a + S]),
                                            dst=view(T[dst + suffix][:, z:z + S])))
                total["sent"] = total.get("sent", 0) + len(engines)
            g.remote_dma_fused(ts, local_sem=T.sem.sent)

    def products(w, home, land, i, blocks, reads):
        k, n, off, width = PIECE[i]
        first = 4 if i == 0 or (i == 2 and land == "a") else 0
        if i < 2:
            PE.wait_ge(T.sem[("far_", "near_")[i] + land], arrive[i])
        near = (land, HC, HC + 128, 0, ["apadq", "apads"]) if land == "a" else (land, 3 * S - 128, 3 * S, 128 - S, [])
        x, a, z, skip, more = [(land, 0, HC, 0, []), near, (home + "2", 0, 128, off, [home + "2q"])][i]
        for j, b in enumerate(blocks):
            mm(first + b, w, 128 * b, x, a, z, reads + more, (w, i, j // 2))
        return first, skip, 16 * k + off, width

    pick("ur", "u")
    pack_half("x", 0, [XT[0]])
    op("v", lambda: V.tensor_copy(T.l_p[:, 0:1], T.cxt[:, 96:97]), ["cxt"], ["l_p"])
    listed(T.l_d[:, 0:1], 0, 0, C + CP - 1, "l_d0", "v1")
    listed(T.l_d[:, 1:2], 0, 256, C + CP - 1, "l_d1", "v1")
    pack_half("x", 1, [XT[1]])
    for j in range(2):
        op("v", lambda: V.tensor_scalar(T.l_rep[:, 16 * j:16 * j + 16], T.cx[:, 0:32].indirect(T.l_p[:, 0:1]), 256.0 * j, C + CP - 1.0, A.add, A.min),
           ["l_p"], ["l_rep%d" % j], "v1")
    scores("ur", "x", 0, 4)
    scores("ur", "x", 1, 6)
    op("v", lambda: V.tensor_scalar(T.after[:], T.cidx[:], T.cxt[:, 32:33], None, A.is_gt), ["cidx", "cxt"], ["after"], "v2")
    pad = 0 if down else CP - 16
    op("y", lambda: g.sync.dma_start(u8(T.a_q[:, 3 * S:3 * S + 16]), u8(T.x_q[:, pad:pad + 16])), ["xq0"], ["apadq"], "apad", load=True)
    op("y", lambda: g.sync.dma_start(T.a_s[:, 3 * S:3 * S + 16], T.x_s[:, pad:pad + 16]), ["xq0"], ["apads"], "apad", load=True)
    sorter(0)[2]()

    XS = [(T.xt[:, 64:64 + WIN], XT)] + [(T["x%d" % b][:, 0:WIN], ["x%d" % b]) for b in (1, 2, 3)]

    def sort_x(q, b, i):
        k, n = PIECE[i][0:2]
        k += 2 * (k // HB)
        move(q, elem(T["ft%d" % i], b, 0, 16 * n), XS[b][0].indirect(T.order1[:, k:k + n]), XS[b][1] + ["order1%d" % (k // 16)], ["ft%d%d" % (i, b)],
             "ft%d" % i, "vs")

    def pack(name, i):
        quant("%s%d" % (name, i), T["%st%d" % (name, i)], 0, 16 * PIECE[i][1], ["%st%d%d" % (name, i, b) for b in range(4)], ["%s%dq" % (name, i)])

    for q, b, i in (("v", 0, 1), ("s", 1, 1), ("v", 2, 1), ("s", 3, 1), ("v", 0, 0)):
        sort_x(q, b, i)
    pack("f", 1)
    send("f", "a", 1)
    for q, b, i in (("s", 1, 0), ("s", 3, 0), ("v", 2, 0), ("v", 0, 2)):
        sort_x(q, b, i)
    pack("f", 0)
    send("f", "a", 0)
    for b in (1, 2, 3):
        sort_x("s", b, 2)
    pack("f", 2)
    quant("v", T.vt, 0, 128, ["vt"], ["vq"])
    quant("e", T.et, 0, 512, ["et%d" % b for b in range(4)], ["eq_"])
    pick("vr", "v")
    fill(T.half[:], 0.5, ["half"], None)

    HT = ["ht%d%d" % (i, b) for i in range(3) for b in range(4)]

    def layer(i):
        first, skip, a, n = products("w", "f", "a", i, range(4), ["wq", "ws"])
        for b in range(4):
            out, src = elem(T.ht, b, 16 + a, 16 + a + n), bank(first + b, skip, skip + n)
            keys = (["ps%d" % (first + b)], ["ht%d%d" % (i, b)], "ht%d" % i, "vs")
            if b % 2:
                op("v", lambda: V.tensor_scalar(out, src, 0.00390625, None, A.mult), *keys)
            else:
                op("s", lambda: SC.activation(out, src, F.Identity, scale=0.00390625), *keys)

    first_signs, first_equal, rest = sorter(1)
    layer(2)
    layer(1)
    pack_half("h", 0, HT[4:])
    layer(0)
    scores("vr", "h", 0, 0)
    first_signs()
    pack_half("h", 1, HT[:4])
    first_equal()
    scores("vr", "h", 1, 2)
    for b in (1, 3, 2):
        op("y", lambda: g.sync.dma_start(T["h%d" % b][:, 0:WIN], T.ht[:, 64 + b:64 + b + WIN]), HT + ["htpad1"], ["h%d" % b], "hcopy", load=True)
    rest()
    order_values(0, "oaf")
    store_order("oaf", T.oa, [])

    HS = [(T.ht[:, 64:64 + WIN], HT)] + [(T["h%d" % b][:, 0:WIN], ["h%d" % b]) for b in (1, 2, 3)]
    P1, P2 = ["place1v", "place1s"], ["place2v", "place2s"]

    def sort_h(q, b, a, z):
        k = 2 * (a // HB)
        move(q, plane(T.hs, b, 16 * a, 16 * z), HS[b][0].indirect(T.order2[:, a + k:z + k]), HS[b][1] + ["order2%d" % (a // HB)], ["hs%d_%d" % (b, a)],
             "hs%d" % b, "vs")

    def scan(b):
        op("v", lambda: V.tensor_tensor_scan(plane(T.rs, b), T.half[:], plane(T.hs, b), 0.0, A.mult, A.max),
           ["half"] + ["hs%d_%d" % (b, a) for a in (0, 8, HB)], ["rs%d" % b])

    def back(q, b, i):
        k, n = PIECE[i][0:2]
        move(q, elem(T["tt%d" % i], b, 0, 16 * n), plane(T.rs, b).indirect(T.place2[:, k:k + n]), ["rs%d" % b] + P2, ["tt%d%d" % (i, b)],
             "tt%d" % i, "vs")

    for q, b, a, z in (("v", 0, 0, HB), ("s", 1, 0, HB), ("v", 0, HB, KB), ("s", 1, HB, KB), ("s", 3, 0, HB), ("s", 3, HB, KB),
                       ("v", 2, 8, HB), ("v", 2, HB, KB), ("s", 2, 0, 8)):
        sort_h(q, b, a, z)
    for b in (0, 1, 3, 2):
        scan(b)
    for q, b, i in (("s", 0, 0), ("s", 1, 0), ("v", 3, 0), ("v", 2, 0), ("v", 2, 1)):
        back(q, b, i)
    pack("t", 0)
    send("t", "b", 0)
    for q, b, i in (("s", 0, 1), ("s", 1, 1), ("s", 3, 1), ("v", 2, 2)):
        back(q, b, i)
    pack("t", 1)
    send("t", "b", 1)
    for q, b in (("s", 0), ("s", 1), ("v", 3)):
        back(q, b, 2)
    pack("t", 2)
    quant("m", T.mt, 0, 128, ["mt"], ["mq"])
    order_values(1, "obf")

    for i in (2, 0, 1):
        first, skip, a, n = products("e", "t", "b", i, (0, 2, 1, 3), ["eq_"])
        off = PIECE[i][2]
        for b in (0, 1):
            op("v", lambda: V.tensor_tensor(plane(T.zs, b, a, a + n), bank(first + b, skip, skip + n), elem(T["ft%d" % i], b, off, off + n), A.add),
               ["ps%d" % (first + b), "ft%d%d" % (i, b)], ["zs%d%d" % (i, b)], "zs%d" % i, "vs")
        for b in (2, 3):
            move("s", plane(T.zs, b, a, a + n), bank(first + b, skip, skip + n), ["ps%d" % (first + b)], ["zs%d%d" % (i, b)], "zs%d" % i, "vs")
    store_order("obf", T.ob, ["zs10"])

    def store_y(i):
        a, z = 16 * ZP[i], 16 * ZP[i + 1]
        q, dq = ("v", "y") if i == len(ZP) - 2 else ("s", "s")
        move(q, T.yf[:, a:z], bank(4 + i, 0, z - a), ["ps%d" % (4 + i)], ["y%d" % i])
        op(dq, lambda: Q[dq].dma_start(T.y[:, a:z], T.yf[:, a:z]), ["y%d" % i], out=True)

    def home(q, b, i):
        a, z = ZP[i], ZP[i + 1]
        reads, keys = ["zs%d%d" % (j, b) for j in range(3)] + P1, (["zt%d%d" % (i, b)], "zt%d" % i, "vs")
        out, src = elem(T.zt, b, 16 * a, 16 * z), plane(T.zs, b).indirect(T.place1[:, a:z])
        if q == "s":
            move("s", out, src, reads, *keys)
        else:
            op("v", lambda: V.tensor_tensor(out, src, elem(T.xt, b, 16 + 16 * a, 16 + 16 * z), A.add), reads, *keys)

    last = len(ZP) - 2
    for i in range(last + 1):
        for q, b in (("s", 0), ("s", 1), ("v", 2), ("v", 3)):
            if i == 0 or b != 2:
                home(q, b, i)
        if i < last:
            home("v", 2, i + 1)
        a, z = 16 * ZP[i], 16 * ZP[i + 1]
        quant("z", T.zt, a, z, ["zt%d%d" % (i, b) for b in range(4)], ["zq%d" % i])
        mm(4 + i, "m", 0, "z", a, z, ["mq", "zq%d" % i])
        op("y", lambda: g.sync.dma_start(T.oc[:, 4 * a:4 * z], u8(T.z_q[:, a:z])), ["zq%d" % i], out=True)
        if i:
            store_y(i - 1)
    for k in range(4):
        op("s", lambda: SC.dma_start(T.osc[4 * k:4 * k + 4, :], T.z_s[32 * k:32 * k + 4, :]), ["zq%d" % i for i in range(last + 1)], out=True)
    store_y(last)

    g.wait_ge(T.sem.sent, total["sent"])
    for s in sorted(last_on, key=lambda x: last_on[x]):
        if waited.get(s, 0) < total[s]:
            g.wait_ge(T.sem[s], total[s])
    g.wait_ge(T.sem.outs, total["outs"])
